import numpy as np, ml_dtypes
CORES = [23,119,17,113]
N = 4
BF = ml_dtypes.bfloat16
def gentries(a):
    return np.ascontiguousarray(a.reshape(8, 16, -1).transpose(0, 2, 1)).reshape(8, -1)
def gtable(e):
    e = np.asarray(e); return np.ascontiguousarray(e.reshape(8, -1, 16).transpose(0, 2, 1)).reshape(128, -1).astype(np.int32)
NO, D, B, K, RO, TH = 16, 3, 224, 16, 4, 9
V, NB = NO * B, NO + D
def every(z):
    return np.concatenate([z, np.stack([np.roll(z[:, :, d - 1], d, axis=0) for d in range(1, D + 1)], axis=2)], axis=2)
def parts(rng):
    a = rng.integers(0, 256, (N, 8, 15, V)); m = (rng.random((N, 8, V)) < 0.0625).astype(np.int64)
    u = np.argsort(rng.random((N, 8, NB, V)), axis=-1)[..., :16 * B].reshape(N, 8, NB, 16, B)
    e = np.argsort(rng.random((N, 8, NO, B)), axis=-1)[..., :K]
    return a, m, u, np.ascontiguousarray(e)
def firsts(e):
    z = np.zeros((N, 8, V), bool); np.put_along_axis(z, (e + B * np.arange(NO)[:, None]).reshape(N, 8, -1), True, 2)
    return z
def reach(u, e):
    z = np.zeros((N, 8, V), bool); q = np.take_along_axis(u, every(e)[:, :, :, None, :], 4)
    np.put_along_axis(z, q.reshape(N, 8, -1), True, 2)
    return z
def cover(rng):
    o = np.argsort(rng.random((N, V)), axis=-1)
    return np.stack([np.roll(o, -16 * K * c, axis=1) for c in range(NB)], axis=1)
def aim(rng, e, g, o):
    ee = every(e)[:, g]; w = np.zeros((N, NB, 16, B), np.int64)
    for r in range(N):
        for c in range(NB):
            rest = np.ones(B, bool); rest[ee[r, c]] = False
            w[r, c][:, ee[r, c]] = o[r, c, :16 * K].reshape(16, K)
            w[r, c][:, rest] = rng.permutation(o[r, c, 16 * K:])[:16 * (B - K)].reshape(16, B - K)
    return w
def pack(a, m, u, e):
    rec = np.concatenate([a, m[:, :, None]], axis=2).reshape(N, 128, V).astype(np.float32).astype(BF)
    up = np.ascontiguousarray(u.transpose(0, 1, 3, 2, 4).reshape(N, 128, NB * B)).astype(np.int32)
    return {"rec": rec, "up": up, "fr": np.stack([gtable(z.reshape(8, -1)) for z in e])}
def setup_inputs(rng):
    return pack(*parts(rng))
def setup_inputs_room(rng):
    a, m, u, e = parts(rng); c = reach(u, e); z = firsts(e); can = c & ~z; pick = np.zeros((N, 8, V), bool)
    for r in range(N):
        for g in range(8):
            for b in range(NO):
                o = b * B + rng.permutation(np.flatnonzero(can[r, g, b * B:(b + 1) * B])); n = int(rng.choice(np.array([0, 1, K - 1, K, K + 1, B])))
                if r == 0 and b == 0: n = (K, K + 1, B, K - 1, 1, 0, K, K + 1)[g]
                pick[r, g, o[:n]] = True
    a = np.where(c[:, :, None], np.where(pick[:, :, None], rng.integers(150, 256, a.shape), rng.integers(0, 51, a.shape)), a)
    a = np.where(z[:, :, None], rng.integers(100, 111, a.shape), a)
    return pack(a, z.astype(np.int64), u, e)
def setup_inputs_ties(rng):
    a, m, u, e = parts(rng); z = firsts(e)
    lo = np.array([0, 254, 100, 0, 7, 127, 1, 128]).reshape(1, 8, 1, 1); step = np.array([1, 1, 1, 255, 1, 1, 2, 1]).reshape(1, 8, 1, 1)
    p = np.where(z, 0.6, 0.15 + 0.3 * rng.random((N, 8, V)))[:, :, None]
    a = lo + step * (rng.random(a.shape) < p)
    a[:, 1] = np.where((rng.random((N, V)) < 0.6)[:, None], 255, a[:, 1])
    return pack(a, m, u, e)
def setup_inputs_meet(rng):
    a, m, u, e = parts(rng)
    u[:, ::2] = u[:, ::2, :1].copy(); e[:, ::2] = e[:1, ::2, :1].copy()
    i = 1 + np.argsort(rng.random((N, 4, NO, B - 2)), axis=-1)[..., :K - 2]
    e[:, 1::2, :, 2:] = i; e[:, 1::2, :, 0] = 0; e[:, 1::2, :, 1] = B - 1
    base = np.arange(16 * B).reshape(B, 16).T; u[:, 1] = base; u[:, 1, NO:] = base + V - 16 * B
    o = np.argsort((np.arange(V) + rng.integers(0, 16, (N, 1, 1))) % 16 + rng.random((N, 1, V)), axis=-1)
    u[:, 2] = aim(rng, e, 2, np.broadcast_to(o, (N, NB, V)))[:, :1]
    u[:, 3] = aim(rng, e, 3, cover(rng)); z = firsts(e)
    a[:, 3] = np.where(z[:, 3][:, None], rng.integers(0, 51, (N, 15, V)), rng.integers(150, 256, (N, 15, V))); m[:, 3] = 0
    return pack(a, m, u, e)
def setup_inputs_dry(rng):
    a, m, u, e = parts(rng); z = firsts(e); o = rng.permutation(8)
    a[:, o[1]] = np.where(z[:, o[1]][:, None], rng.integers(100, 256, (N, 15, V)), rng.integers(0, 100, (N, 15, V)))
    for g in (o[3], o[4]):
        a[:, g] = np.where(rng.random((N, 15, V)) < 0.7, 255, rng.integers(0, 101, (N, 15, V)))
    a[:, o[3], :, ::B] = 0
    u[:, o[5]] = aim(rng, e, o[5], cover(rng))
    a[:, o[5]] = np.where(z[:, o[5]][:, None], rng.integers(0, 31, (N, 15, V)), rng.integers(80, 256, (N, 15, V)))
    a[:, o[5], :, ::B] = rng.integers(60, 101, (N, 15, NO))
    m[:, o[0]] = 1; m[:, o[2]] = rng.random((N, V)) < 0.9; m[:, o[3]] = 1; m[:, o[4]] = rng.random((N, V)) < 0.95
    m[:, o[5]] = 1; m[:, o[5], ::B] = 0
    m[(rng.integers(-2, 1) + np.arange(3)) % N] = 1
    return pack(a, m, u, e)
def setup_inputs_spread(rng):
    a, m, u, e = parts(rng); s = np.exp2(8.2 * rng.random((N, 8, 1, V)))
    a = np.minimum((s * rng.random(a.shape)).astype(np.int64), 255); m = (rng.random(m.shape) < rng.random((N, 8, 1)) * 0.5).astype(np.int64)
    return pack(a, m, u, e)
def check_inputs(d):
    bad = []
    r = d["rec"].astype(np.float32).reshape(N, 8, 16, V); a, m = r[:, :, :15], r[:, :, 15]
    if not np.all((a >= 0) & (a <= 255) & (a == np.floor(a))): bad.append("notes in rec")
    if not np.all((m == 0) | (m == 1)): bad.append("marks in rec")
    if np.min(d["up"]) < 0 or np.max(d["up"]) > V - 1: bad.append("range of up")
    u = np.sort(d["up"].reshape(N, 8, 16, NB, B).transpose(0, 1, 3, 2, 4).reshape(N, 8, NB, 16 * B), axis=-1)
    if np.any(u[..., 1:] == u[..., :-1]): bad.append("different parents in a bank of up")
    if np.min(d["fr"]) < 0 or np.max(d["fr"]) > B - 1: bad.append("range of fr")
    e = np.sort(np.stack([gentries(z) for z in d["fr"]]).reshape(N, 8, NO, K), axis=-1)
    if np.any(e[..., 1:] == e[..., :-1]): bad.append("different places in a bank of fr")
    return bad
def reference(rec, up, fr):
    s = rec.astype(np.float32).astype(np.int64).reshape(N, 8, 16, V); a = s[:, :, :15].copy(); mark = s[:, :, 15] > 0
    u = up.astype(np.int64).reshape(N, 8, 16, NB, B)
    e = np.stack([gentries(z) for z in fr]).astype(np.int64).reshape(N, 8, NO, K); live = np.ones(e.shape, bool)
    for wave in range(RO):
        node = e + B * np.arange(NO)[:, None]
        x = np.take_along_axis(a, node.reshape(N, 8, 1, NO * K), 3).reshape(N, 8, 15, NO, K)
        ee, ll, xx = every(e), every(live), every(np.moveaxis(x, 2, 3))
        new = a.copy(); hit = np.zeros((N, 8, V), bool)
        for b in range(NB):
            q = np.take_along_axis(u[:, :, :, b], ee[:, :, None, b], 3).reshape(N, 8, 1, 16 * K)
            old = np.take_along_axis(a, q, 3)
            arr = np.tile(xx[:, :, b], (1, 1, 1, 16))
            ok = (np.add.reduce((old >= arr).astype(np.int64), axis=2) >= TH) & np.tile(ll[:, :, b], (1, 1, 16))
            r, g, j = np.nonzero(ok); to = q[r, g, 0, j]
            new[r, g, :, to] = ((old + arr) >> 1)[r, g, :, j]
            hit[r, g, to] = True
        h = (hit & ~mark).reshape(N, 8, NO, B); mark = mark | hit; a = new
        e = np.argsort(~h, axis=-1, kind="stable")[..., :K]; live = np.take_along_axis(h, e, 3)
    return {"y": np.concatenate([a, mark[:, :, None].astype(np.int64)], axis=2).reshape(N, 128, V).astype(np.float32).astype(BF)}

@@ -1,0 +1,393 @@
+from concourse.bass import DstId, RemoteDMATransfer
+from concourse.mybir import AluOpType, AxisListType, ActivationFunctionType
+
+OP, ACT = AluOpType, ActivationFunctionType
+N, B, NO, NB, D, WAVES = 4, 224, 16, 19, 3, 4
+V = NO * B
+S = 240
+W0 = V + 384
+OFF = 4096
+WT = OFF + W0
+PW = 17
+BIG = 8388608.0
+BLOCKS = [(0, 4), (4, 8), (8, 12), (12, 16), (16, 19)]
+LISTS = [(0, 4), (4, 8), (8, 16)]
+GATHER = "avaaa"
+CMP = "aaaavvaaaa"
+VAL = "vaaaaaaaaa"
+CNT = "vvaaaava"
+XG = "vaa"
+XEV = "aaaaa"
+INIT = 1792
+
+SCRATCH = {}
+for _n, _w, _d in (("fr_s", 16, "int32"), ("rb", W0, "bfloat16"), ("a0", WT, "float32"), ("a1", WT, "float32"), ("up_s", NB * S, "int32"),
+                   ("dm", 16, "int32"), ("kI", 8, "int32"), ("kc", 8, "float32"), ("E", 1024, "bfloat16"), ("EG", 768, "bfloat16"),
+                   ("HI", 128, "bfloat16"), ("NI", 128, "bfloat16"), ("WS", 144, "bfloat16"), ("RM", 2048, "bfloat16"),
+                   ("XT", 128 * 8, "bfloat16"), ("TU", 16, "float32"), ("TN", 16, "float32"), ("TG", 8, "float32"), ("f0", 256, "bfloat16"),
+                   ("f1", 256, "float32"), ("f2", 256, "float32"), ("f3", 256, "float32"), ("rk", S, "bfloat16"), ("junk", NO * S, "bfloat16"),
+                   ("sums", 16, "float32"), ("tu", 32, "float32"), ("tn", 32, "float32"), ("lu", 32, "uint16"), ("ln", 32, "uint16"),
+                   ("q16", 16 * NB, "uint16"), ("qs", 16 * NB, "float32"), ("x", 16 * NO, "bfloat16"), ("old", 256 * NB, "bfloat16"),
+                   ("cb", 256 * NB, "bfloat16"), ("val", 256 * NB, "float32"), ("of", 16 * NB, "float32"), ("o16", 16 * NB, "uint16"),
+                   ("yb", V, "bfloat16")):
+    SCRATCH[_n] = ("sbuf", [128, _w], _d)
+for _i in range(WAVES):
+    SCRATCH["snd%d" % _i] = ("sbuf", [128, D * PW], "bfloat16")
+    SCRATCH["rcv%d" % _i] = ("sbuf", [128, D * PW], "bfloat16")
+PSUM = ["p0", "p1", "p2", "p3", "r0", "r1", "px", "pc"]
+for _n in PSUM:
+    SCRATCH[_n] = ("psum", [128, 512], "float32")
+SEMAPHORES = ["sv", "sa", "sp", "sg", "sent"] + ["gh%d" % i for i in range(WAVES)] + ["d%d" % i for i in range(40)]
+
+SEED, NOISE = 660, 0.0
+CYC = 1e-3
+GA, SC, PECYC, HOP, LAT, BW, DLAT, EPS = 1.5, 2.0, 0.7e-3, 0.12, 10.0, 200e3, 1.8, 0.1
+
+
+def R(buf, lo, hi, step=1, p0=0, p1=128):
+    return (buf, lo, hi, step, p0, p1)
+
+
+def ap(T, r):
+    if r[0] == "at":
+        return ap(T, r[1]).indirect(ap(T, r[2]))
+    b, lo, hi, step, p0, p1 = r
+    return T[b][p0:p1, lo:hi] if step == 1 else T[b][p0:p1, lo:hi:step]
+
+
+def width(r):
+    return 16 * width(r[2]) if r[0] == "at" else -(-(r[2] - r[1]) // r[3])
+
+
+def plan():
+    ops, hist = [], {}
+
+    def access(i, r, kind):
+        if r[0] == "at":
+            access(i, r[1], kind)
+            access(i, r[2], "r")
+            return
+        buf, lo, hi = r[0], r[1], r[2]
+        deps, psum = ops[i]["deps"], buf in PSUM
+        if psum:
+            lo, hi = 0, 512
+        keep = []
+        for (l, h, j, k) in hist.get(buf, []):
+            if j != i and l < hi and lo < h and (psum or kind == "w" or k == "w"):
+                a, b = ops[j], ops[i]
+                if a["q"] == "p" and b["q"] == "p":
+                    deps.setdefault(j, False)
+                else:
+                    deps[j] = deps.get(j, False) or k == "w" or a["dma"] > 0 or b["dma"] > 0 or a["q"] != b["q"]
+            if not (lo <= l and h <= hi and kind == "w" and j != i):
+                keep.append((l, h, j, k))
+        hist[buf] = keep + [(lo, hi, i, kind)]
+
+    def add(q, fn, reads, writes, cost, dma=0, lat=0.0):
+        ops.append({"q": q, "fn": fn, "cost": cost, "dma": dma, "lat": lat, "deps": {}})
+        for r in reads:
+            access(len(ops) - 1, r, "r")
+        for r in writes:
+            access(len(ops) - 1, r, "w")
+
+    def cy(out, in_, k=1.0):
+        k = SC if out[0] == "at" else (GA if in_[0] == "at" else k)
+        return 0.055 + max(64, width(in_) * k) * CYC
+
+    def load(q, out, name, rows, lo, hi, size):
+        add(q, lambda g, T: (g.sync if q == "s" else g.scalar).dma_start(ap(T, out), T[name][rows, lo:hi]), [], [out], 0.06, size)
+
+    def move(out, in_, size):
+        add("s", lambda g, T: g.sync.dma_start(ap(T, out), ap(T, in_)), [in_], [out], 0.06, size)
+
+    def fill(r, x):
+        add("v", lambda g, T: g.vector.memset(ap(T, r), x), [], [r], cy(r, r, 0.5))
+
+    def copy(q, out, in_, bias=0.0):
+        if q == "v":
+            add("v", lambda g, T: g.vector.tensor_copy(ap(T, out), ap(T, in_)), [in_], [out], cy(out, in_))
+        else:
+            add("a", lambda g, T: g.scalar.activation(ap(T, out), ap(T, in_), ACT.Copy, bias=bias), [in_], [out], cy(out, in_))
+
+    def scal(out, in_, a, b, o0, o1=None):
+        reads = [in_] + ([a] if isinstance(a, tuple) else [])
+        if o1 is None:
+            add("v", lambda g, T: g.vector.tensor_scalar(ap(T, out), ap(T, in_), ap(T, a) if isinstance(a, tuple) else a, None, o0), reads, [out], cy(out, in_))
+        else:
+            add("v", lambda g, T: g.vector.tensor_scalar(ap(T, out), ap(T, in_), ap(T, a) if isinstance(a, tuple) else a, b, o0, o1), reads, [out], cy(out, in_))
+
+    def both(out, x, y, op, k=2.0):
+        add("v", lambda g, T: g.vector.tensor_tensor(ap(T, out), ap(T, x), ap(T, y), op), [x, y], [out], cy(out, x, k))
+
+    def sign(out, in_, bias, scale, acc=None):
+        reads = [in_] + ([bias] if isinstance(bias, tuple) else [])
+        add("a", lambda g, T: g.scalar.activation(ap(T, out), ap(T, in_), ACT.Sign, bias=ap(T, bias) if isinstance(bias, tuple) else bias, scale=scale,
+                                                  accum_out=ap(T, acc) if acc else None), reads, [out] + ([acc] if acc else []), cy(out, in_) + 0.02)
+
+    def mm(out, lhs, rhs, start, stop):
+        add("p", lambda g, T: g.tensor.matmul(ap(T, out), ap(T, lhs), ap(T, rhs), start, stop), [lhs, rhs], [out], 0.03 + max(64, width(rhs)) * PECYC)
+
+    def pick(r, pat, op, x, base, cm):
+        add("g", lambda g, T: g.affine_select(ap(T, r), ap(T, r), pat, op, x, base, cm), [r], [r], 0.17 + 2 * CYC * width(r))
+
+    def iota(r, pat, base, cm):
+        add("g", lambda g, T: g.iota(ap(T, r), pat, base, cm, allow_small_or_imprecise_dtypes=True), [], [r], 0.13 + 2 * CYC * width(r))
+
+    every = slice(0, 128)
+    load("s", R("fr_s", 0, 16), "fr", every, 0, 16, 8192)
+    load("s", R("rb", 0, V), "rec", every, 0, V, 256 * V)
+    for b in range(NB):
+        load("sa"[b % 2], R("up_s", b * S, b * S + B), "up", every, b * B, b * B + B, 512 * B)
+    load("s", R("f0", 0, B), "rec", slice(15, 128, 16), 0, V, 57344)
+
+    fill(R("rb", V, W0), 0.0)
+    iota(R("dm", 0, 16), [[16, 16]], V, 1)
+    for (tb, st) in (("TU", 2 * S), ("TN", 2 * B)):
+        if "v" in CNT:
+            iota(R(tb, 0, 16), [[st, 16]], 0, 0)
+        for p in range(8):
+            if CNT[p] == "a" and (p == 0 or CNT[p - 1] != "a"):
+                e = p
+                while e < 8 and CNT[e] == "a":
+                    e += 1
+                iota(R(tb, 2 * p, 2 * e), [[st, 2 * (e - p)]], 2 * p * st + S, 0)
+    fill(R("HI", 0, 128), 0.5)
+    pick(R("HI", 0, 128), [[-1, 128]], OP.is_equal, 0.0, 0, 1)
+    pick(R("HI", 0, 128), [[0, 8], [1, 16]], OP.not_equal, 0.0, -15, 0)
+    fill(R("E", 0, 1024), 1.0)
+    pick(R("E", 0, 1024, 1, 0, 64), [[1, 1024]], OP.is_ge, 0.0, 0, -16)
+    pick(R("E", 0, 1024, 1, 0, 64), [[-1, 1024]], OP.is_ge, 0.0, 15, 16)
+    scal(R("NI", 0, 128), R("HI", 0, 128), -1.0, None, OP.mult)
+    NX = 128 * len(BLOCKS)
+    fill(R("XT", 0, NX), -0.25)
+    pick(R("XT", 0, NX), [[0, NX // 16], [1, 16]], OP.not_equal, 1.0, -15, 0)
+    fill(R("XT", 0, NX, 1, 0, 64), 0.0)
+    fill(R("WS", 0, 144), 1.0)
+    pick(R("WS", 0, 144), [[0, 9], [1, 16]], OP.is_equal, 0.0, -15, 0)
+    pick(R("WS", 0, 144), [[-16, 9], [0, 16]], OP.is_ge, 0.0, 0, 1)
+    pick(R("WS", 0, 144), [[16, 9], [0, 16]], OP.is_ge, 0.0, 14, -1)
+    iota(R("TG", 0, D), [[S, D]], S * NO, 0)
+    fill(R("EG", 0, 768), 1.0)
+    pick(R("EG", 0, 768, 1, 0, 64), [[16 * PW, D], [1, 256]], OP.is_ge, 0.0, 0, -16)
+    pick(R("EG", 0, 768, 1, 0, 64), [[-16 * PW, D], [-1, 256]], OP.is_ge, 0.0, 15, 16)
+    fill(R("RM", 0, 2048), 1.0)
+    pick(R("RM", 0, 2048), [[-1, 16], [-16, 8], [0, 16]], OP.is_equal, 0.0, 0, 1)
+    iota(R("kI", 0, 1), [[0, 1]], 0, 1)
+    scal(R("kI", 1, 2), R("kI", 0, 1), 15, None, OP.bitwise_and)
+    copy("v", R("kc", 0, 1), R("kI", 1, 2))
+    scal(R("kc", 1, 2), R("kI", 1, 2), 0.5, None, OP.add)
+    for b in range(NB):
+        copy("v", R("up_s", b * S + B, b * S + S), R("dm", 0, 16))
+    fill(R("a0", OFF + V, WT), 0.0)
+    copy("v", R("a0", OFF, OFF + INIT), R("rb", 0, INIT))
+    copy("a", R("a0", OFF + INIT, OFF + V), R("rb", INIT, V))
+    for w in range(WAVES):
+        fill(R("f%d" % w, B, S), float(w))
+    fill(R("a1", OFF + V, WT), 0.0)
+    rot = {"p": 0, "r": 0}
+
+    def tile(kind, n):
+        rot[kind] += 1
+        return kind + str((rot[kind] - 1) % n)
+
+    def wave(w):
+        src = R("rb", 0, W0) if w == 0 else R("a%d" % ((w - 1) % 2), OFF, WT)
+        dst, snd, rcv = "a%d" % (w % 2), "snd%d" % w, "rcv%d" % w
+        if w == 0:
+            for p in range(8):
+                c = (2 * p, 2 * p + 2)
+                if CNT[p] == "a":
+                    scal(R("sums", *c), R("fr_s", *c), 2.0, float(-S), OP.mult, OP.add)
+                else:
+                    scal(R("sums", *c), R("fr_s", *c), 2.0, None, OP.mult)
+        else:
+            fn, fo = R("f%d" % w, 0, S), R("f%d" % (w - 1), 0, S)
+            add("v", lambda g, T: g.vector.tensor_tensor_scan(T.rk[:, :], ap(T, fn), ap(T, fo), 0.0, OP.add, OP.subtract), [fn, fo], [R("rk", 0, S)], 0.3)
+            for p in range(8):
+                t = tile("r", 2)
+                for h in range(2):
+                    b = 2 * p + h
+                    mm(R(t, h * S, h * S + S), R("RM", b * 128, b * 128 + 128), R("rk", 0, S), True, True)
+                if CNT[p] == "v":
+                    scal(R("junk", 2 * p * S, 2 * p * S + 2 * S), R(t, 0, 2 * S), R("kc", 0, 1), 2.0, OP.is_le, OP.mult)
+                for h in range(2):
+                    b = 2 * p + h
+                    jk, sm = R("junk", b * S, b * S + S), R("sums", b, b + 1)
+                    if CNT[p] == "a":
+                        sign(jk, R(t, h * S, h * S + S), R("kc", 1, 2), -1.0, sm)
+                    else:
+                        add("v", lambda g, T, jk=jk, sm=sm: g.vector.tensor_reduce(ap(T, sm), ap(T, jk), AxisListType.X, OP.add), [jk], [sm], 0.3)
+
+        def lists(lo, hi, xq):
+            for (tm, tb, ls) in (("tu", "TU", "lu"), ("tn", "TN", "ln")):
+                both(R(tm, lo, hi), R("sums", lo, hi), R(tb, lo, hi), OP.add)
+                scal(R(ls, lo, hi), R(tm, lo, hi), 0.5, None, OP.mult)
+            q = R("q16", lo * 16, hi * 16)
+            copy("v", q, ("at", R("up_s", 0, hi * S), R("lu", lo, hi)))
+            copy(xq, R("x", lo * 16, hi * 16), ("at", src, R("ln", lo, hi)))
+            scal(R("qs", lo * 16, hi * 16), q, 64.0, None, OP.add)
+
+        def block(k, m, buf, lo):
+            mm(R("px", 0, 128, 1, 0, m), R(buf, lo, lo + m), R("HI", 0, 128), True, True)
+            copy(XEV[k], R("XT", k * 128, k * 128 + 128, 1, 0, m), R("px", 0, 128, 1, 0, m))
+
+        def unit(u):
+            k, (b0, b1) = u, BLOCKS[u]
+            lo, hi, n = b0 * 256, b1 * 256, 16 * (b1 - b0)
+            l16, h16 = b0 * 16, b1 * 16
+            copy(GATHER[u], R("old", lo, hi), ("at", src, R("q16", l16, h16)))
+            for b in range(b0, b1, 2):
+                a, z = b * 256, min(b + 2, b1) * 256
+                m, eo = z - a, (b - b0) * 256
+                od, cq = R("old", a, z), CMP[b // 2]
+                xt, ex = R("XT", k * 128, k * 128 + 128, 1, 0, 65), R("EG" if b0 == NO else "E", eo, eo + m, 1, 0, 65)
+                if cq == "a":
+                    t = R(tile("p", 4), 0, m)
+                    mm(t, xt, ex, True, False)
+                    mm(t, R("NI", 0, 128), od, False, True)
+                    sign(R("cb", a, z), t, 0.0, -1.0)
+                t = R(tile("p", 4), 0, m)
+                mm(t, xt, ex, True, False)
+                mm(t, R("HI", 0, 128), od, False, True)
+                if cq == "v":
+                    both(R("cb", a, z), od, t, OP.is_gt, 1.0)
+                if VAL[b // 2] == "a":
+                    copy("a", R("val", a, z), t, BIG)
+                else:
+                    scal(R("val", a, z), t, BIG, None, OP.add)
+
+            def count(g, T):
+                for i in range(16):
+                    r = g.tensor.matmul(T.pc[:, 0:n], T.WS[:, 15 - i:143 - i], T.cb[:, lo + i:hi:16], i == 0, i == 15)
+                return r
+            add("p", count, [R("cb", lo, hi), R("WS", 0, 144)], [R("pc", 0, n)], 16 * (0.01 + max(64, n) * PECYC))
+            sign(R("pc", 256, 256 + n), R("pc", 0, n), -2.0 if CMP[b0 // 2] == "a" else -8.5, 1.0)
+            both(R("of", l16, h16), R("pc", 256, 256 + n), R("qs", l16, h16), OP.mult, 1.0)
+            scal(R("o16", l16, h16), R("of", l16, h16), float(OFF - 64), None, OP.add)
+            for b in range(b0, b1):
+                scal(("at", R(dst, 0, WT), R("o16", b * 16, b * 16 + 16)), R("val", b * 256, b * 256 + 256), 1.0, -BIG, OP.mult, OP.add)
+
+        done = 0
+        for (li, (lo, hi)) in enumerate(LISTS):
+            lists(lo, hi, XG[li])
+            if lo < D <= hi:
+                for (l, h) in ((0, 2), (2, D)):
+                    scal(R(snd, l * PW + 16, h * PW, PW), R("sums", l, h), 0.5, (S / 2 if CNT[l // 2] == "a" else 0.0), OP.mult, OP.add)
+                for d in range(D):
+                    o, i = R(snd, d * PW, d * PW + 16), R("x", d * 16, d * 16 + 16)
+                    add("g", lambda g, T, o=o, i=i: g.affine_select(ap(T, o), ap(T, i), [[0, 16]], OP.is_equal, 0.0, 0, 0), [i], [o], 0.2)
+                add("g", w, [R(snd, 0, D * PW)], [R(rcv, 0, D * PW)], 1.5, 0, LAT)
+            while BLOCKS[done][1] <= hi:
+                block(done, 16 * (BLOCKS[done][1] - BLOCKS[done][0]), "x", BLOCKS[done][0] * 16)
+                unit(done)
+                done += 1
+        both(R("tu", 16, 16 + D), R(rcv, 16, D * PW, PW), R("TG", 0, D), OP.add)
+        copy("v", R("lu", 16, 16 + D), R("tu", 16, 16 + D))
+        copy("v", R("q16", 256, 304), ("at", R("up_s", 0, NB * S), R("lu", 16, 16 + D)))
+        scal(R("qs", 256, 304), R("q16", 256, 304), 64.0, None, OP.add)
+        block(done, D * PW, rcv, 0)
+        unit(done)
+        if w < WAVES - 1:
+            o = R("f%d" % (w + 1), 0, B)
+            add("s", lambda g, T: g.sync.dma_start(ap(T, o), T[dst][15::16, OFF:OFF + V]), [R(dst, OFF, OFF + V)], [o], 0.06, 114688)
+            move(R("a%d" % ((w + 1) % 2), OFF, OFF + V), R(dst, OFF, OFF + V), 512 * V)
+            ops[-1]["deps"].setdefault(len(ops) - 2, False)
+        else:
+            for j in range(4):
+                lo, hi = j * (V // 4), (j + 1) * (V // 4)
+                o = R("yb", lo, hi)
+                copy("va"[j % 2], o, R(dst, OFF + lo, OFF + hi))
+                add("s", lambda g, T, o=o: g.sync.dma_start(T.y[:, o[1]:o[2]], ap(T, o)), [o], [], 0.06, 64 * V)
+
+    for w in range(WAVES):
+        wave(w)
+    return ops
+
+
+def order(ops):
+    n = len(ops)
+    succ, need = [[] for _ in ops], [len(o["deps"]) for o in ops]
+    for i, o in enumerate(ops):
+        for j in o["deps"]:
+            succ[j].append(i)
+    bl, rs = [0.0] * n, SEED
+    for i in range(n - 1, -1, -1):
+        o = ops[i]
+        rs = (rs * 1103515245 + 12345) % 2147483648
+        bl[i] = (rs / 2147483648.0 - 0.5) * NOISE + o["cost"] + o["lat"] + (DLAT + o["dma"] / BW if o["dma"] else 0.0) + max([bl[j] + HOP for j in succ[i]] + [0.0])
+    free, dma, rt = {q: 0.0 for q in "vapgs"}, 0.0, [0.0] * n
+    ready = {q: [i for i in range(n) if need[i] == 0 and ops[i]["q"] == q] for q in "vapgs"}
+    out = []
+    while len(out) < n:
+        e, q = min((min(max(free[q], rt[i]) for i in ready[q]), q) for q in "vapgs" if ready[q])
+        i = max([i for i in ready[q] if max(free[q], rt[i]) <= e + EPS], key=lambda i: (bl[i], -i))
+        ready[q].remove(i)
+        o = ops[i]
+        free[q] = max(free[q], rt[i]) + o["cost"]
+        end = free[q] + o["lat"]
+        if o["dma"]:
+            end = dma = max(dma, free[q] + DLAT) + o["dma"] / BW
+        out.append(i)
+        for j in succ[i]:
+            rt[j] = max(rt[j], end + HOP if ops[j]["deps"][i] else free[q])
+            need[j] -= 1
+            if need[j] == 0:
+                ready[ops[j]["q"]].append(j)
+    return out
+
+
+def rank_program(g, core, T, topo):
+    rank = T.rank_of(core)
+    if rank is None:
+        return
+    ops = plan()
+    seq = order(ops)
+    queue = {"v": g.vector, "a": g.scalar, "p": g.tensor, "g": g, "s": g.sync}
+    watched, last = [False] * len(ops), {}
+    for o in ops:
+        for j, must in o["deps"].items():
+            watched[j] = watched[j] or must
+    for i in seq:
+        last[ops[i]["q"]] = i
+    dsts, eng, used = [T.cores[(rank + d) % N] for d in range(1, D + 1)], {}, []
+    for z in sorted(dsts, key=lambda z: len(topo.engines(core, z))):
+        eng[z] = [e for e in topo.engines(core, z) if e not in used][:4]
+        used = used + eng[z]
+    tok, total, waited, seen, nd = {}, {}, {}, {}, 0
+    for i in seq:
+        o, req = ops[i], {}
+        q = o["q"]
+        for j, must in o["deps"].items():
+            if must:
+                s, v = tok[j]
+                req[s] = max(req.get(s, 0), v)
+        for s in sorted(req):
+            if seen.get((q, s), 0) < req[s]:
+                queue[q].wait_ge(T.sem[s], req[s])
+                seen[(q, s)] = req[s]
+                waited[s] = max(waited.get(s, 0), req[s])
+        if isinstance(o["fn"], int):
+            w, tr = o["fn"], []
+            for d, z in enumerate(dsts):
+                rid, pid, _ = topo.addr(z)
+                tr.append(RemoteDMATransfer(dst_ids=[DstId(rid=rid, pnc=pid)], dma_engine_mask=sum(1 << e for e in eng[z]), remote_sem=T.sem["gh%d" % w],
+                                            src=T["snd%d" % w][:, d * PW:d * PW + PW], dst=T["rcv%d" % w][:, d * PW:d * PW + PW]))
+            g.remote_dma_fused(tr, local_sem=T.sem.sent)
+            total["sent"] = total.get("sent", 0) + sum(len(eng[z]) for z in dsts)
+            tok[i] = ("gh%d" % w, 4 * D)
+            total["gh%d" % w] = 4 * D
+            continue
+        r = o["fn"](g, T)
+        if o["dma"]:
+            s, nd = "d%d" % nd, nd + 1
+            r.then_inc(T.sem[s], 16)
+            total[s] = 16
+            tok[i] = (s, 16)
+        elif watched[i] or last[q] == i:
+            s = "s" + q
+            total[s] = total.get(s, 0) + 1
+            r.then_inc(T.sem[s], 1)
+            tok[i] = (s, total[s])
+    for s in total:
+        if waited.get(s, 0) < total[s]:
+            g.wait_ge(T.sem[s], total[s])

@@ -1,47 +1,57 @@
 from concourse.bass import DstId, RemoteDMATransfer
-from concourse.mybir import AluOpType, AxisListType, ActivationFunctionType
+from concourse.mybir import AluOpType, ActivationFunctionType
 
 OP, ACT = AluOpType, ActivationFunctionType
 N, B, NO, NB, D, WAVES = 4, 224, 16, 19, 3, 4
 V = NO * B
-S = 240
 W0 = V + 384
-OFF = 4096
-WT = OFF + W0
+GH = V + 16
+UP = GH + D * B + 16
+BL = B // 16
 PW = 17
 BIG = 8388608.0
-BLOCKS = [(0, 4), (4, 8), (8, 12), (12, 16), (16, 19)]
-LISTS = [(0, 4), (4, 8), (8, 16)]
-GATHER = "avaaa"
-CMP = "aaaavvaaaa"
-VAL = "vaaaaaaaaa"
-CNT = "vvaaaava"
-XG = "vaa"
+GROUPS = [(0, 4, "px", "pc", 0), (4, 16, "p2", "p2", 512)]
+UNITS = [(0, 2, "vvv", None, ("p0", 0)), (2, 4, "aaa", ("p1", 0), ("p1", 512)), (4, 8, "aaa", ("p2", 0), ("p0", 0)),
+         (8, 12, "aaa", ("p1", 0), ("p2", 0)), (12, 16, "aaa", ("p0", 0), ("p1", 0)), (16, 19, "aaa", ("p2", 0), ("p0", 0))]
+COPY = [(0, 448, "v"), (448, 896, "a"), (896, 1600, "v"), (1600, 2816, "a"), (2816, V, "g")]
+FILL = "avav"
+LAST = "vavavava"
+PEV = "vaa"
+XG = "aaa"
 XEV = "aaaaa"
-INIT = 1792
+QF = "v"
+ORDER = ["""place0 list0 place1 x0 fill0 ghostE send later turn0 xt0 fill2 tell fill1 q0 old2 diff2 list1 x1 turn1 xt1 cmp2 qf0 old0 sum0 fill3 q4 qf4
+old4 cmp0 latest val0 count0.0 sum2 turn2 count0.1 aim0 put0 q8 diff4 val2 xt2 old8 cmp4 count2.0 count2.1 put1 sum4 val4 aim2 put2 count4.0 turn3
+count4.1 diff8 qf8 put3 q12 old12 aim4 xt3 cmp8 count8.0 sum8 val8 diff12 cmp12 count8.1 qf12 put4 heard put5 q16 put6 put7 old16 aim8 put8 put9 put10
+turn4 xt4 count12.0 sum12 val12 count12.1 aim12 diff16 cmp16 put11 qf16 sum16 val16 count16.0 count16.1 marks0 put12 put13 put14 aim16 marks1.0 marks1.4
+marks1.8 marks1.12 keep1 put15 put16 put17 put18 keep0""",
+         """copy4 copy0 copy2 copy1 copy3 marks0 keep0 runs0 marks1.0 marks1.4 marks1.8 marks1.12 keep1 cum0 le0 run0 empty0 place0.0 runlist0 rank0 runs1
+within0 place0.2 cum1 le1 rank1 run1 empty1 list0 x0 place1.0 send runlist1 tell q0 turn0 within1 place1.2 old0 list1 q4 old2 xt0 sum0 x1 qf0 old4 cmp0
+val0 qf4 sum2 count0.0 turn1 xt1 count0.1 diff2 val2 cmp2 aim0 diff4 put0 put1 old8 cmp4 count2.0 count2.1 aim2 put2 turn2 xt2 sum4 val4 put3 count4.0
+count4.1 aim4 put4 put5 diff8 old12 cmp8 sum8 turn3 xt3 count8.0 count8.1 heard put6 q16 val8 old16 put7 aim8 put8 qf16 diff12 cmp12 sum12 turn4 xt4
+count12.0 count12.1 diff16 val12 cmp16 sum16 val16 put9 put10 put11 aim12 put12 count16.0 count16.1 put13 put14 aim16 put15 put16 put17 put18"""]
 
 SCRATCH = {}
-for _n, _w, _d in (("fr_s", 16, "int32"), ("rb", W0, "bfloat16"), ("a0", WT, "float32"), ("a1", WT, "float32"), ("up_s", NB * S, "int32"),
-                   ("dm", 16, "int32"), ("kI", 8, "int32"), ("kc", 8, "float32"), ("E", 1024, "bfloat16"), ("EG", 768, "bfloat16"),
-                   ("HI", 128, "bfloat16"), ("NI", 128, "bfloat16"), ("WS", 144, "bfloat16"), ("RM", 2048, "bfloat16"),
-                   ("XT", 128 * 8, "bfloat16"), ("TU", 16, "float32"), ("TN", 16, "float32"), ("TG", 8, "float32"), ("f0", 256, "bfloat16"),
-                   ("f1", 256, "float32"), ("f2", 256, "float32"), ("f3", 256, "float32"), ("rk", S, "bfloat16"), ("junk", NO * S, "bfloat16"),
-                   ("sums", 16, "float32"), ("tu", 32, "float32"), ("tn", 32, "float32"), ("lu", 32, "uint16"), ("ln", 32, "uint16"),
-                   ("q16", 16 * NB, "uint16"), ("qs", 16 * NB, "float32"), ("x", 16 * NO, "bfloat16"), ("old", 256 * NB, "bfloat16"),
-                   ("cb", 256 * NB, "bfloat16"), ("val", 256 * NB, "float32"), ("of", 16 * NB, "float32"), ("o16", 16 * NB, "uint16"),
-                   ("yb", V, "bfloat16")):
+for _n, _w, _d in (("fr_s", 16, "int32"), ("rb", W0, "bfloat16"), ("wn", 2 * W0, "float32"), ("up_s", UP, "int32"),
+                   ("kI", 8, "int32"), ("kc", 8, "float32"), ("E", 1024, "bfloat16"), ("EG", 768, "bfloat16"), ("ID", 128, "bfloat16"),
+                   ("HI", 128, "bfloat16"), ("NI", 128, "bfloat16"), ("HF", 128, "float32"), ("I64", 128, "float32"), ("I16", 128, "bfloat16"),
+                   ("WS", 144, "bfloat16"), ("W2", 144, "bfloat16"), ("WM", 144, "bfloat16"), ("AP", 128, "bfloat16"), ("AN", 128, "bfloat16"),
+                   ("LP", 128, "bfloat16"), ("LN", 128, "bfloat16"), ("MK", B, "bfloat16"), ("CB", B, "bfloat16"), ("KC", 256, "bfloat16"),
+                   ("TJ", 16, "float32"), ("J", 16, "float32"), ("TB", 16, "float32"), ("XT", 128 * 5, "bfloat16"),
+                   ("m0", B, "bfloat16"), ("m1", B, "bfloat16"), ("cum", B, "bfloat16"), ("le", B, "bfloat16"), ("hi", B, "bfloat16"),
+                   ("rk", B, "bfloat16"), ("i16", 16, "uint16"), ("c2", 256, "bfloat16"), ("ej", 16, "float32"), ("tu", 16, "float32"),
+                   ("lu", 32, "uint16"), ("q16", 16 * NB, "uint16"), ("qf", 16 * NB, "float32"), ("x", 16 * NO, "bfloat16"),
+                   ("old", 256 * NB, "bfloat16"), ("cb", 256 * NB, "bfloat16"), ("val", 256 * NB, "float32"), ("o16", 16 * NB, "uint16")):
     SCRATCH[_n] = ("sbuf", [128, _w], _d)
 for _i in range(WAVES):
-    SCRATCH["snd%d" % _i] = ("sbuf", [128, D * PW], "bfloat16")
-    SCRATCH["rcv%d" % _i] = ("sbuf", [128, D * PW], "bfloat16")
-PSUM = ["p0", "p1", "p2", "p3", "r0", "r1", "px", "pc"]
+    SCRATCH["snd%d" % _i] = ("sbuf", [128, D * PW], "float32")
+    SCRATCH["rcv%d" % _i] = ("sbuf", [128, D * PW], "float32")
+PSUM = {"p0": 1024, "p1": 1024, "p2": 1024, "px": 512, "pc": 512}
 for _n in PSUM:
-    SCRATCH[_n] = ("psum", [128, 512], "float32")
-SEMAPHORES = ["sv", "sa", "sp", "sg", "sent"] + ["gh%d" % i for i in range(WAVES)] + ["d%d" % i for i in range(40)]
+    SCRATCH[_n] = ("psum", [128, PSUM[_n]], "float32")
+SEMAPHORES = ["sv", "sa", "sp", "sg", "sent"] + ["gh%d" % i for i in range(WAVES)] + ["d%d" % i for i in range(24)]
 
-SEED, NOISE = 660, 0.0
-CYC = 1e-3
-GA, SC, PECYC, HOP, LAT, BW, DLAT, EPS = 1.5, 2.0, 0.7e-3, 0.12, 10.0, 200e3, 1.8, 0.1
+COST = {"cyc": 1e-3, "ga": 1.5, "sc": 3.0, "pe": 0.5e-3, "mm": 0.02, "hop": 0.12, "lat": 5.0, "call": 1.5, "bw": 200e3, "dlat": 1.8, "eps": 0.1}
 
 
 def R(buf, lo, hi, step=1, p0=0, p1=128):
@@ -59,8 +69,19 @@ def width(r):
     return 16 * width(r[2]) if r[0] == "at" else -(-(r[2] - r[1]) // r[3])
 
 
+def narrow(*rs):
+    return all(SCRATCH[r[0]][2] in ("bfloat16", "uint16") for r in rs)
+
+
+def message(T, U, w, d):
+    return T["snd%d" % w][:, d * PW:d * PW + PW], U["rcv%d" % w][:, d * PW:d * PW + PW]
+
+
 def plan():
-    ops, hist = [], {}
+    ops, hist, C, now = [], {}, COST, [0, "start"]
+
+    def step(name, i=""):
+        now[1] = name + str(i)
 
     def access(i, r, kind):
         if r[0] == "at":
@@ -70,7 +91,7 @@ def plan():
         buf, lo, hi = r[0], r[1], r[2]
         deps, psum = ops[i]["deps"], buf in PSUM
         if psum:
-            lo, hi = 0, 512
+            lo, hi = lo // 512 * 512, -(-hi // 512) * 512
         keep = []
         for (l, h, j, k) in hist.get(buf, []):
             if j != i and l < hi and lo < h and (psum or kind == "w" or k == "w"):
@@ -79,260 +100,278 @@ def plan():
                     deps.setdefault(j, False)
                 else:
                     deps[j] = deps.get(j, False) or k == "w" or a["dma"] > 0 or b["dma"] > 0 or a["q"] != b["q"]
-            if not (lo <= l and h <= hi and kind == "w" and j != i):
+            if not (lo <= l and h <= hi and kind == "w" and j != i and r[3] == 1):
                 keep.append((l, h, j, k))
         hist[buf] = keep + [(lo, hi, i, kind)]
 
     def add(q, fn, reads, writes, cost, dma=0, lat=0.0):
-        ops.append({"q": q, "fn": fn, "cost": cost, "dma": dma, "lat": lat, "deps": {}})
+        ops.append({"q": q, "fn": fn, "cost": cost, "dma": dma, "lat": lat, "deps": {}, "at": tuple(now)})
         for r in reads:
             access(len(ops) - 1, r, "r")
         for r in writes:
             access(len(ops) - 1, r, "w")
 
     def cy(out, in_, k=1.0):
-        k = SC if out[0] == "at" else (GA if in_[0] == "at" else k)
-        return 0.055 + max(64, width(in_) * k) * CYC
+        k = C["sc"] if out[0] == "at" else (C["ga"] if in_[0] == "at" else k)
+        return 0.055 + max(64, width(in_) * k) * C["cyc"]
 
-    def load(q, out, name, rows, lo, hi, size):
-        add(q, lambda g, T: (g.sync if q == "s" else g.scalar).dma_start(ap(T, out), T[name][rows, lo:hi]), [], [out], 0.06, size)
+    def half(out, in_):
+        return 0.5 if out[0] != "at" and in_[0] != "at" and narrow(out, in_) else 1.0
 
-    def move(out, in_, size):
-        add("s", lambda g, T: g.sync.dma_start(ap(T, out), ap(T, in_)), [in_], [out], 0.06, size)
+    def load(q, out, name, lo, hi, size):
+        add(q, lambda g, T: (g.sync if q == "s" else g.scalar).dma_start(ap(T, out), T[name][:, lo:hi]), [], [out], 0.06, size)
 
     def fill(r, x):
         add("v", lambda g, T: g.vector.memset(ap(T, r), x), [], [r], cy(r, r, 0.5))
 
     def copy(q, out, in_, bias=0.0):
         if q == "v":
-            add("v", lambda g, T: g.vector.tensor_copy(ap(T, out), ap(T, in_)), [in_], [out], cy(out, in_))
-        else:
+            add("v", lambda g, T: g.vector.tensor_copy(ap(T, out), ap(T, in_)), [in_], [out], cy(out, in_, half(out, in_)))
+        elif q == "a":
             add("a", lambda g, T: g.scalar.activation(ap(T, out), ap(T, in_), ACT.Copy, bias=bias), [in_], [out], cy(out, in_))
+        else:
+            n = width(out)
+            add("g", lambda g, T: g.affine_select(ap(T, out), ap(T, in_), [[0, n]], OP.is_equal, 0.0, 0, 0), [in_], [out], 0.17 + 2 * C["cyc"] * n)
 
     def scal(out, in_, a, b, o0, o1=None):
-        reads = [in_] + ([a] if isinstance(a, tuple) else [])
-        if o1 is None:
-            add("v", lambda g, T: g.vector.tensor_scalar(ap(T, out), ap(T, in_), ap(T, a) if isinstance(a, tuple) else a, None, o0), reads, [out], cy(out, in_))
-        else:
-            add("v", lambda g, T: g.vector.tensor_scalar(ap(T, out), ap(T, in_), ap(T, a) if isinstance(a, tuple) else a, b, o0, o1), reads, [out], cy(out, in_))
+        reads, more = [in_] + ([a] if isinstance(a, tuple) else []), ([] if o1 is None else [o1])
+        add("v", lambda g, T: g.vector.tensor_scalar(ap(T, out), ap(T, in_), ap(T, a) if isinstance(a, tuple) else a, b, o0, *more), reads, [out],
+            cy(out, in_, half(out, in_)))
 
     def both(out, x, y, op, k=2.0):
         add("v", lambda g, T: g.vector.tensor_tensor(ap(T, out), ap(T, x), ap(T, y), op), [x, y], [out], cy(out, x, k))
 
-    def sign(out, in_, bias, scale, acc=None):
-        reads = [in_] + ([bias] if isinstance(bias, tuple) else [])
-        add("a", lambda g, T: g.scalar.activation(ap(T, out), ap(T, in_), ACT.Sign, bias=ap(T, bias) if isinstance(bias, tuple) else bias, scale=scale,
-                                                  accum_out=ap(T, acc) if acc else None), reads, [out] + ([acc] if acc else []), cy(out, in_) + 0.02)
+    def scan(out, x, y, o0, o1):
+        add("v", lambda g, T: g.vector.tensor_tensor_scan(ap(T, out), ap(T, x), ap(T, y), 0.0, o0, o1), [x, y], [out], cy(out, y, half(out, y)))
 
-    def mm(out, lhs, rhs, start, stop):
-        add("p", lambda g, T: g.tensor.matmul(ap(T, out), ap(T, lhs), ap(T, rhs), start, stop), [lhs, rhs], [out], 0.03 + max(64, width(rhs)) * PECYC)
+    def sign(out, in_):
+        add("a", lambda g, T: g.scalar.activation(ap(T, out), ap(T, in_), ACT.Sign, bias=0.0, scale=-1.0), [in_], [out], cy(out, in_))
+
+    def mm(*terms, cut=()):
+        name = now[1]
+        for lo, hi in zip((0,) + cut, cut + (len(terms),)):
+            def fn(g, T, lo=lo, hi=hi):
+                for i in range(lo, hi):
+                    r = g.tensor.matmul(*[ap(T, z) for z in terms[i]], i == 0, i == len(terms) - 1)
+                return r
+            cost = sum(C["mm"] + max(64, width(t[2])) * C["pe"] * (1 if narrow(t[2]) else 4) for t in terms[lo:hi])
+            step(name, "." + str(lo) if cut else "")
+            add("p", fn, [r for t in terms[lo:hi] for r in t[1:]], [terms[0][0]], cost)
+        step(name)
 
     def pick(r, pat, op, x, base, cm):
-        add("g", lambda g, T: g.affine_select(ap(T, r), ap(T, r), pat, op, x, base, cm), [r], [r], 0.17 + 2 * CYC * width(r))
+        add("g", lambda g, T: g.affine_select(ap(T, r), ap(T, r), pat, op, x, base, cm), [r], [r], 0.17 + 2 * C["cyc"] * width(r))
 
     def iota(r, pat, base, cm):
-        add("g", lambda g, T: g.iota(ap(T, r), pat, base, cm, allow_small_or_imprecise_dtypes=True), [], [r], 0.13 + 2 * CYC * width(r))
+        add("g", lambda g, T: g.iota(ap(T, r), pat, base, cm, allow_small_or_imprecise_dtypes=True), [], [r], 0.13 + 2 * C["cyc"] * width(r))
 
-    every = slice(0, 128)
-    load("s", R("fr_s", 0, 16), "fr", every, 0, 16, 8192)
-    load("s", R("rb", 0, V), "rec", every, 0, V, 256 * V)
-    for b in range(NB):
-        load("sa"[b % 2], R("up_s", b * S, b * S + B), "up", every, b * B, b * B + B, 512 * B)
-    load("s", R("f0", 0, B), "rec", slice(15, 128, 16), 0, V, 57344)
+    def nodes(lo, hi):
+        return R("wn", 2 * lo + 1, 2 * hi, 2)
 
+    load("s", R("fr_s", 0, 16), "fr", 0, 16, 8192)
+    load("a", R("up_s", 0, 4 * B), "up", 0, 4 * B, 2048 * B)
+    for j in range(4):
+        load("s", R("rb", j * V // 4, (j + 1) * V // 4), "rec", j * V // 4, (j + 1) * V // 4, 64 * V)
+    for b in range(4, NO, 4):
+        load("s", R("up_s", b * B, (b + 4) * B), "up", b * B, (b + 4) * B, 2048 * B)
+    load("s", R("up_s", GH, GH + D * B), "up", V, V + D * B, 512 * D * B)
+
+    whole = lambda n: R(n, 0, SCRATCH[n][1][1])
+    for n, x in (("ID", 1.0), ("E", 1.0), ("AP", 1.0), ("EG", 1.0), ("WS", 0.0), ("WM", 0.0), ("MK", 1.0), ("XT", -0.25)):
+        fill(whole(n), x)
     fill(R("rb", V, W0), 0.0)
-    iota(R("dm", 0, 16), [[16, 16]], V, 1)
-    for (tb, st) in (("TU", 2 * S), ("TN", 2 * B)):
-        if "v" in CNT:
-            iota(R(tb, 0, 16), [[st, 16]], 0, 0)
-        for p in range(8):
-            if CNT[p] == "a" and (p == 0 or CNT[p - 1] != "a"):
-                e = p
-                while e < 8 and CNT[e] == "a":
-                    e += 1
-                iota(R(tb, 2 * p, 2 * e), [[st, 2 * (e - p)]], 2 * p * st + S, 0)
-    fill(R("HI", 0, 128), 0.5)
-    pick(R("HI", 0, 128), [[-1, 128]], OP.is_equal, 0.0, 0, 1)
-    pick(R("HI", 0, 128), [[0, 8], [1, 16]], OP.not_equal, 0.0, -15, 0)
-    fill(R("E", 0, 1024), 1.0)
-    pick(R("E", 0, 1024, 1, 0, 64), [[1, 1024]], OP.is_ge, 0.0, 0, -16)
-    pick(R("E", 0, 1024, 1, 0, 64), [[-1, 1024]], OP.is_ge, 0.0, 15, 16)
-    scal(R("NI", 0, 128), R("HI", 0, 128), -1.0, None, OP.mult)
-    NX = 128 * len(BLOCKS)
-    fill(R("XT", 0, NX), -0.25)
-    pick(R("XT", 0, NX), [[0, NX // 16], [1, 16]], OP.not_equal, 1.0, -15, 0)
-    fill(R("XT", 0, NX, 1, 0, 64), 0.0)
-    fill(R("WS", 0, 144), 1.0)
-    pick(R("WS", 0, 144), [[0, 9], [1, 16]], OP.is_equal, 0.0, -15, 0)
-    pick(R("WS", 0, 144), [[-16, 9], [0, 16]], OP.is_ge, 0.0, 0, 1)
-    pick(R("WS", 0, 144), [[16, 9], [0, 16]], OP.is_ge, 0.0, 14, -1)
-    iota(R("TG", 0, D), [[S, D]], S * NO, 0)
-    fill(R("EG", 0, 768), 1.0)
-    pick(R("EG", 0, 768, 1, 0, 64), [[16 * PW, D], [1, 256]], OP.is_ge, 0.0, 0, -16)
-    pick(R("EG", 0, 768, 1, 0, 64), [[-16 * PW, D], [-1, 256]], OP.is_ge, 0.0, 15, 16)
-    fill(R("RM", 0, 2048), 1.0)
-    pick(R("RM", 0, 2048), [[-1, 16], [-16, 8], [0, 16]], OP.is_equal, 0.0, 0, 1)
+    iota(whole("TB"), [[B, NO]], 0, 0)
     iota(R("kI", 0, 1), [[0, 1]], 0, 1)
+    pick(whole("ID"), [[-1, 128]], OP.is_equal, 0.0, 0, 1)
+    pick(whole("AP"), [[-16, 8], [0, 16]], OP.is_ge, 0.0, 0, 1)
+    pick(whole("AP"), [[16, 8], [0, 16]], OP.is_ge, 0.0, 15, -1)
+    pick(R("E", 0, 1024, 1, 0, 64), [[1, 64], [0, 16]], OP.is_equal, 0.0, 0, -1)
+    iota(R("up_s", UP - 16, UP), [[16, 16]], V, 1)
+    fill(R("XT", 15, 640, 16), 1.0)
+    fill(R("MK", 0, B, BL), 0.0)
     scal(R("kI", 1, 2), R("kI", 0, 1), 15, None, OP.bitwise_and)
+    fill(R("XT", 0, 640, 1, 0, 64), 0.0)
+    scal(whole("HI"), whole("ID"), 0.5, None, OP.mult)
     copy("v", R("kc", 0, 1), R("kI", 1, 2))
-    scal(R("kc", 1, 2), R("kI", 1, 2), 0.5, None, OP.add)
-    for b in range(NB):
-        copy("v", R("up_s", b * S + B, b * S + S), R("dm", 0, 16))
-    fill(R("a0", OFF + V, WT), 0.0)
-    copy("v", R("a0", OFF, OFF + INIT), R("rb", 0, INIT))
-    copy("a", R("a0", OFF + INIT, OFF + V), R("rb", INIT, V))
-    for w in range(WAVES):
-        fill(R("f%d" % w, B, S), float(w))
-    fill(R("a1", OFF + V, WT), 0.0)
-    rot = {"p": 0, "r": 0}
+    scal(R("kc", 1, 2), R("kI", 1, 2), float(D * B), None, OP.add)
+    fill(R("HI", 15, 128, 16), 0.0)
+    scal(whole("I64"), whole("ID"), 64.0, None, OP.mult)
+    scal(whole("I16"), whole("ID"), 16.0, None, OP.mult)
+    scal(whole("NI"), whole("HI"), -1.0, None, OP.mult)
+    copy("v", whole("HF"), whole("HI"))
+    copy("v", R("WM", 15, 128, 16), R("ID", 15, 128, 16))
+    copy("v", R("WS", 15, 128, 16), R("AP", 15, 128, 16))
+    scal(whole("AN"), whole("AP"), -1.0, None, OP.mult)
+    copy("v", whole("LP"), whole("AP"))
+    scal(whole("W2"), whole("WS"), 2.0, None, OP.mult)
+    step("ghostE")
+    pick(R("EG", 0, 768, 1, 0, 64), [[PW, D], [1, 16], [0, 16]], OP.is_equal, 0.0, 0, -1)
+    step("later")
+    iota(R("up_s", V, GH), [[16, 16]], V, 1)
+    pick(whole("LP"), [[-1, 128]], OP.is_gt, 0.0, 0, 1)
+    iota(whole("CB"), [[BL, NO], [0, BL]], 0, 0)
+    iota(whole("KC"), [[0, NO], [1, 16]], 0, 0)
+    iota(whole("TJ"), [[-B, NO]], V - B, 0)
+    step("latest")
+    scal(whole("LN"), whole("LP"), -1.0, None, OP.mult)
+    scal(whole("J"), whole("TJ"), R("kc", 0, 1), 1.0 / 64, OP.add, OP.mult)
+    for j in range(4):
+        step("fill", j)
+        copy(FILL[j], nodes(j * V // 4, (j + 1) * V // 4), R("rb", j * V // 4, (j + 1) * V // 4))
 
-    def tile(kind, n):
-        rot[kind] += 1
-        return kind + str((rot[kind] - 1) % n)
+    def marks(w, gi):
+        b0, b1, t = GROUPS[gi][:3]
+        o = R(t, 0, BL * (b1 - b0))
+        step("marks", gi)
+        mm(*[(o, R("WM", 15 - j, 143 - j), R("rb", b0 * B + j, b1 * B, 16)) for j in range(16)], cut=(4, 8, 12) if gi else ())
+        step("keep", gi)
+        copy(PEV[gi], R("m%d" % (w % 2), b0 * BL, b1 * BL), o)
+
+    def frontier(w, gi):
+        b0, b1, t, t2, at = GROUPS[gi]
+        lo, hi, n = b0 * BL, b1 * BL, BL * (b1 - b0)
+        new, was = R("m%d" % (w % 2), lo, hi), R("m%d" % ((w - 1) % 2), lo, hi)
+        tot, rest = R(t2, at, at + n), R(t2, at + 256, at + 256 + n)
+        step("runs", gi)
+        mm((tot, whole("AN"), was), (tot, whole("AP"), new))
+        mm((rest, whole("LP"), was), (rest, whole("LN"), new))
+        step("cum", gi)
+        scan(R("cum", lo, hi), R("MK", lo, hi), tot, OP.mult, OP.add)
+        step("le", gi)
+        scal(R("le", lo, hi), R("cum", lo, hi), R("kc", 0, 1), None, OP.is_le)
+        step("rank", gi)
+        both(R("rk", lo, hi), rest, R("cum", lo, hi), OP.add, 1.0)
+        step("run", gi)
+        scan(R("hi", lo, hi), R("CB", lo, hi), R("le", lo, hi), OP.max, OP.add)
+        run = R("hi", lo + BL - 2, hi, BL)
+        step("runlist", gi)
+        copy("v", R("i16", b0, b1), run)
+        step("empty", gi)
+        both(R("ej", b0, b1), R("le", lo + BL - 1, hi, BL), R("J", b0, b1), OP.mult)
+        step("within", gi)
+        both(R("c2", b0 * 16, b1 * 16), ("at", R("rk", 0, hi), R("i16", b0, b1)), R("KC", b0 * 16, b1 * 16), OP.is_le)
+        o = R(t, 0, b1 - b0)
+        step("place", gi)
+        mm(*([(o, whole("I16"), run), (o, whole("I64"), R("ej", b0, b1))]
+             + [(o, R("WS", 15 - k, 143 - k), R("c2", b0 * 16 + k, b1 * 16, 16)) for k in range(16)]), cut=(2,))
+        return o
 
     def wave(w):
-        src = R("rb", 0, W0) if w == 0 else R("a%d" % ((w - 1) % 2), OFF, WT)
-        dst, snd, rcv = "a%d" % (w % 2), "snd%d" % w, "rcv%d" % w
-        if w == 0:
-            for p in range(8):
-                c = (2 * p, 2 * p + 2)
-                if CNT[p] == "a":
-                    scal(R("sums", *c), R("fr_s", *c), 2.0, float(-S), OP.mult, OP.add)
-                else:
-                    scal(R("sums", *c), R("fr_s", *c), 2.0, None, OP.mult)
-        else:
-            fn, fo = R("f%d" % w, 0, S), R("f%d" % (w - 1), 0, S)
-            add("v", lambda g, T: g.vector.tensor_tensor_scan(T.rk[:, :], ap(T, fn), ap(T, fo), 0.0, OP.add, OP.subtract), [fn, fo], [R("rk", 0, S)], 0.3)
-            for p in range(8):
-                t = tile("r", 2)
-                for h in range(2):
-                    b = 2 * p + h
-                    mm(R(t, h * S, h * S + S), R("RM", b * 128, b * 128 + 128), R("rk", 0, S), True, True)
-                if CNT[p] == "v":
-                    scal(R("junk", 2 * p * S, 2 * p * S + 2 * S), R(t, 0, 2 * S), R("kc", 0, 1), 2.0, OP.is_le, OP.mult)
-                for h in range(2):
-                    b = 2 * p + h
-                    jk, sm = R("junk", b * S, b * S + S), R("sums", b, b + 1)
-                    if CNT[p] == "a":
-                        sign(jk, R(t, h * S, h * S + S), R("kc", 1, 2), -1.0, sm)
-                    else:
-                        add("v", lambda g, T, jk=jk, sm=sm: g.vector.tensor_reduce(ap(T, sm), ap(T, jk), AxisListType.X, OP.add), [jk], [sm], 0.3)
+        src, snd, rcv = whole("rb"), "snd%d" % w, "rcv%d" % w
+        now[0] = w
 
-        def lists(lo, hi, xq):
-            for (tm, tb, ls) in (("tu", "TU", "lu"), ("tn", "TN", "ln")):
-                both(R(tm, lo, hi), R("sums", lo, hi), R(tb, lo, hi), OP.add)
-                scal(R(ls, lo, hi), R(tm, lo, hi), 0.5, None, OP.mult)
+        def parents(lo, hi, win):
             q = R("q16", lo * 16, hi * 16)
-            copy("v", q, ("at", R("up_s", 0, hi * S), R("lu", lo, hi)))
-            copy(xq, R("x", lo * 16, hi * 16), ("at", src, R("ln", lo, hi)))
-            scal(R("qs", lo * 16, hi * 16), q, 64.0, None, OP.add)
+            step("q", lo)
+            copy("v", q, ("at", win, R("lu", lo, hi)))
+            step("qf", lo)
+            copy(QF, R("qf", lo * 16, hi * 16), q)
 
-        def block(k, m, buf, lo):
-            mm(R("px", 0, 128, 1, 0, m), R(buf, lo, lo + m), R("HI", 0, 128), True, True)
+        def turn(k, m, buf, lo, by):
+            step("turn", k)
+            mm((R("px", 0, 128, 1, 0, m), R(buf, lo, lo + m), whole(by)))
+            step("xt", k)
             copy(XEV[k], R("XT", k * 128, k * 128 + 128, 1, 0, m), R("px", 0, 128, 1, 0, m))
 
-        def unit(u):
-            k, (b0, b1) = u, BLOCKS[u]
-            lo, hi, n = b0 * 256, b1 * 256, 16 * (b1 - b0)
-            l16, h16 = b0 * 16, b1 * 16
-            copy(GATHER[u], R("old", lo, hi), ("at", src, R("q16", l16, h16)))
-            for b in range(b0, b1, 2):
-                a, z = b * 256, min(b + 2, b1) * 256
-                m, eo = z - a, (b - b0) * 256
-                od, cq = R("old", a, z), CMP[b // 2]
-                xt, ex = R("XT", k * 128, k * 128 + 128, 1, 0, 65), R("EG" if b0 == NO else "E", eo, eo + m, 1, 0, 65)
-                if cq == "a":
-                    t = R(tile("p", 4), 0, m)
-                    mm(t, xt, ex, True, False)
-                    mm(t, R("NI", 0, 128), od, False, True)
-                    sign(R("cb", a, z), t, 0.0, -1.0)
-                t = R(tile("p", 4), 0, m)
-                mm(t, xt, ex, True, False)
-                mm(t, R("HI", 0, 128), od, False, True)
-                if cq == "v":
-                    both(R("cb", a, z), od, t, OP.is_gt, 1.0)
-                if VAL[b // 2] == "a":
-                    copy("a", R("val", a, z), t, BIG)
-                else:
-                    scal(R("val", a, z), t, BIG, None, OP.add)
+        def unit(b0, b1, qs, pd, ps):
+            k, lo, hi, n = b0 // 4, b0 * 256, b1 * 256, 16 * (b1 - b0)
+            l16, h16, m = b0 * 16, b1 * 16, hi - lo
+            od = R("old", lo, hi)
+            step("old", b0)
+            copy(qs[0], od, ("at", src, R("q16", l16, h16)))
 
-            def count(g, T):
-                for i in range(16):
-                    r = g.tensor.matmul(T.pc[:, 0:n], T.WS[:, 15 - i:143 - i], T.cb[:, lo + i:hi:16], i == 0, i == 15)
-                return r
-            add("p", count, [R("cb", lo, hi), R("WS", 0, 144)], [R("pc", 0, n)], 16 * (0.01 + max(64, n) * PECYC))
-            sign(R("pc", 256, 256 + n), R("pc", 0, n), -2.0 if CMP[b0 // 2] == "a" else -8.5, 1.0)
-            both(R("of", l16, h16), R("pc", 256, 256 + n), R("qs", l16, h16), OP.mult, 1.0)
-            scal(R("o16", l16, h16), R("of", l16, h16), float(OFF - 64), None, OP.add)
+            def spread(t, at, by):
+                for a in range(0, m, 512):
+                    z, eo = min(a + 512, m), (b0 % 4) * 256
+                    o = R(t, at + a, at + z)
+                    mm((o, R("XT", k * 128, k * 128 + 128, 1, 0, 65), R("EG" if b0 == NO else "E", eo + a, eo + z, 1, 0, 65)), (o, whole(by), R("old", lo + a, lo + z)))
+                return R(t, at, at + m)
+            if qs[1] == "a":
+                step("diff", b0)
+                s = spread(*pd, "NI")
+                step("cmp", b0)
+                sign(R("cb", lo, hi), s)
+            step("sum", b0)
+            s = spread(*ps, "HI")
+            if qs[1] == "v":
+                step("cmp", b0)
+                both(R("cb", lo, hi), od, s, OP.is_gt, 1.0)
+            step("val", b0)
+            if qs[2] == "a":
+                copy("a", R("val", lo, hi), s, BIG)
+            else:
+                scal(R("val", lo, hi), s, BIG, None, OP.add)
+            o = R("pc", 0, n)
+            step("count", b0)
+            mm(*([(o, whole("I64"), R("qf", l16, h16))] + [(o, R("WS" if qs[1] == "a" else "W2", 15 - i, 143 - i), R("cb", lo + i, hi, 16)) for i in range(16)]), cut=(1,))
+            step("aim", b0)
+            scal(R("o16", l16, h16), o, 1.0 / 32, (15.0 if qs[1] == "a" else -1.0) / 32, OP.mult, OP.add)
             for b in range(b0, b1):
-                scal(("at", R(dst, 0, WT), R("o16", b * 16, b * 16 + 16)), R("val", b * 256, b * 256 + 256), 1.0, -BIG, OP.mult, OP.add)
+                step("put", b)
+                scal(("at", whole("wn"), R("o16", b * 16, b * 16 + 16)), R("val", b * 256, b * 256 + 256), 1.0, -BIG, OP.mult, OP.add)
 
-        done = 0
-        for (li, (lo, hi)) in enumerate(LISTS):
-            lists(lo, hi, XG[li])
-            if lo < D <= hi:
-                for (l, h) in ((0, 2), (2, D)):
-                    scal(R(snd, l * PW + 16, h * PW, PW), R("sums", l, h), 0.5, (S / 2 if CNT[l // 2] == "a" else 0.0), OP.mult, OP.add)
+        for j, (lo, hi, q) in enumerate(COPY if w else []):
+            step("copy", j)
+            copy(q, R("rb", lo, hi), nodes(lo, hi))
+        for gi, (b0, b1, _, _, _) in enumerate(GROUPS):
+            if w == 0:
+                node = R("tu", b0, b1)
+                step("place", gi)
+                both(node, R("fr_s", b0, b1), R("TB", b0, b1), OP.add)
+            else:
+                marks(w, gi)
+                node = frontier(w, gi)
+            step("list", gi)
+            copy("v", R("lu", b0, b1), node)
+            for b in range(b0, b1, 4 if w == 0 else NO):
+                z = min(b + 4, b1) if w == 0 else b1
+                parents(b, z, R("up_s", 0, GH if w else z * B))
+            step("x", gi)
+            copy(XG[gi], R("x", b0 * 16, b1 * 16), ("at", src if w else R("rb", 0, b1 * B), R("lu", b0, b1)))
+            if b0 == 0:
+                step("tell")
+                scal(R(snd, 16, D * PW, PW), R(node[0], node[1], node[1] + D), R("kc", 1, 2), None, OP.min)
+                step("send")
                 for d in range(D):
-                    o, i = R(snd, d * PW, d * PW + 16), R("x", d * 16, d * 16 + 16)
-                    add("g", lambda g, T, o=o, i=i: g.affine_select(ap(T, o), ap(T, i), [[0, 16]], OP.is_equal, 0.0, 0, 0), [i], [o], 0.2)
-                add("g", w, [R(snd, 0, D * PW)], [R(rcv, 0, D * PW)], 1.5, 0, LAT)
-            while BLOCKS[done][1] <= hi:
-                block(done, 16 * (BLOCKS[done][1] - BLOCKS[done][0]), "x", BLOCKS[done][0] * 16)
-                unit(done)
-                done += 1
-        both(R("tu", 16, 16 + D), R(rcv, 16, D * PW, PW), R("TG", 0, D), OP.add)
-        copy("v", R("lu", 16, 16 + D), R("tu", 16, 16 + D))
-        copy("v", R("q16", 256, 304), ("at", R("up_s", 0, NB * S), R("lu", 16, 16 + D)))
-        scal(R("qs", 256, 304), R("q16", 256, 304), 64.0, None, OP.add)
-        block(done, D * PW, rcv, 0)
-        unit(done)
-        if w < WAVES - 1:
-            o = R("f%d" % (w + 1), 0, B)
-            add("s", lambda g, T: g.sync.dma_start(ap(T, o), T[dst][15::16, OFF:OFF + V]), [R(dst, OFF, OFF + V)], [o], 0.06, 114688)
-            move(R("a%d" % ((w + 1) % 2), OFF, OFF + V), R(dst, OFF, OFF + V), 512 * V)
-            ops[-1]["deps"].setdefault(len(ops) - 2, False)
-        else:
-            for j in range(4):
-                lo, hi = j * (V // 4), (j + 1) * (V // 4)
-                o = R("yb", lo, hi)
-                copy("va"[j % 2], o, R(dst, OFF + lo, OFF + hi))
-                add("s", lambda g, T, o=o: g.sync.dma_start(T.y[:, o[1]:o[2]], ap(T, o)), [o], [], 0.06, 64 * V)
+                    copy("g", R(snd, d * PW, d * PW + 16), R("x", d * 16, d * 16 + 16))
+                add("g", w, [whole(snd)], [whole(rcv)], C["call"], 0, C["lat"])
+            for u in UNITS:
+                if b0 <= u[0] < b1:
+                    if u[0] % 4 == 0:
+                        turn(u[0] // 4, 64, "x", u[0] * 16, "HI")
+                    unit(*u)
+        step("heard")
+        copy("v", R("lu", NO, NB), R(rcv, 16, D * PW, PW))
+        parents(NO, NB, R("up_s", GH, UP))
+        turn(4, D * PW, rcv, 0, "HF")
+        unit(*UNITS[-1])
+        if w == 0:
+            for gi in range(len(GROUPS)):
+                marks(0, gi)
 
     for w in range(WAVES):
         wave(w)
+    now[0] = WAVES
+    for j, q in enumerate(LAST):
+        lo, hi = j * V // len(LAST), (j + 1) * V // len(LAST)
+        o = R("rb", lo, hi)
+        copy(q, o, nodes(lo, hi))
+        add("s", lambda g, T, o=o: g.sync.dma_start(T.y[:, o[1]:o[2]], ap(T, o)), [o], [], 0.06, 256 * (hi - lo))
     return ops
 
 
 def order(ops):
-    n = len(ops)
-    succ, need = [[] for _ in ops], [len(o["deps"]) for o in ops]
-    for i, o in enumerate(ops):
-        for j in o["deps"]:
-            succ[j].append(i)
-    bl, rs = [0.0] * n, SEED
-    for i in range(n - 1, -1, -1):
-        o = ops[i]
-        rs = (rs * 1103515245 + 12345) % 2147483648
-        bl[i] = (rs / 2147483648.0 - 0.5) * NOISE + o["cost"] + o["lat"] + (DLAT + o["dma"] / BW if o["dma"] else 0.0) + max([bl[j] + HOP for j in succ[i]] + [0.0])
-    free, dma, rt = {q: 0.0 for q in "vapgs"}, 0.0, [0.0] * n
-    ready = {q: [i for i in range(n) if need[i] == 0 and ops[i]["q"] == q] for q in "vapgs"}
-    out = []
-    while len(out) < n:
-        e, q = min((min(max(free[q], rt[i]) for i in ready[q]), q) for q in "vapgs" if ready[q])
-        i = max([i for i in ready[q] if max(free[q], rt[i]) <= e + EPS], key=lambda i: (bl[i], -i))
-        ready[q].remove(i)
-        o = ops[i]
-        free[q] = max(free[q], rt[i]) + o["cost"]
-        end = free[q] + o["lat"]
-        if o["dma"]:
-            end = dma = max(dma, free[q] + DLAT) + o["dma"] / BW
+    def turn(i):
+        w, name = ops[i]["at"]
+        names = ORDER[min(w, 1)].split() if w < WAVES else []
+        return (w, names.index(name) if name in names else -1, i)
+    out, left = [], sorted(range(len(ops)), key=turn)
+    done = set()
+    while left:
+        i = [i for i in left if done.issuperset(ops[i]["deps"])][0]
+        left.remove(i)
+        done.add(i)
         out.append(i)
-        for j in succ[i]:
-            rt[j] = max(rt[j], end + HOP if ops[j]["deps"][i] else free[q])
-            need[j] -= 1
-            if need[j] == 0:
-                ready[ops[j]["q"]].append(j)
     return out
 
 
@@ -370,8 +409,9 @@ def rank_program(g, core, T, topo):
             w, tr = o["fn"], []
             for d, z in enumerate(dsts):
                 rid, pid, _ = topo.addr(z)
+                src, dst = message(T, T, w, d)
                 tr.append(RemoteDMATransfer(dst_ids=[DstId(rid=rid, pnc=pid)], dma_engine_mask=sum(1 << e for e in eng[z]), remote_sem=T.sem["gh%d" % w],
-                                            src=T["snd%d" % w][:, d * PW:d * PW + PW], dst=T["rcv%d" % w][:, d * PW:d * PW + PW]))
+                                            src=src, dst=dst))
             g.remote_dma_fused(tr, local_sem=T.sem.sent)
             total["sent"] = total.get("sent", 0) + sum(len(eng[z]) for z in dsts)
             tok[i] = ("gh%d" % w, 4 * D)

@@ -5,43 +5,44 @@ OP, ACT = AluOpType, ActivationFunctionType
 N, B, NO, NB, D, WAVES = 4, 224, 16, 19, 3, 4
 V = NO * B
 W0 = V + 384
-GH = V + 16
-UP = GH + D * B + 16
+OFF = 4096
+S = B + 16
+F = 4
+M0 = 16 * F
+GH = M0 + V + 16
+UP = GH + D * S
 BL = B // 16
 PW = 17
-BIG = 8388608.0
-GROUPS = [(0, 4, "px", "pc", 0), (4, 16, "p2", "p2", 512)]
-UNITS = [(0, 2, "vvv", None, ("p0", 0)), (2, 4, "aaa", ("p1", 0), ("p1", 512)), (4, 8, "aaa", ("p2", 0), ("p0", 0)),
+BIG = 2.0 ** 23
+HUGE = BIG * OFF
+ROWS = [BIG, HUGE, -HUGE]
+FRESH = [("p0", 0), ("p0", 512), ("p1", 0), ("p1", 512), ("px", 0), ("pc", 0)]
+UNITS = [(0, 2, "avv", None, ("p0", 0)), (2, 4, "aav", ("p1", 0), ("p1", 512)), (4, 8, "aaa", ("p2", 0), ("p0", 0)),
          (8, 12, "aaa", ("p1", 0), ("p2", 0)), (12, 16, "aaa", ("p0", 0), ("p1", 0)), (16, 19, "aaa", ("p2", 0), ("p0", 0))]
-COPY = [(0, 448, "v"), (448, 896, "a"), (896, 1600, "v"), (1600, 2816, "a"), (2816, V, "g")]
-FILL = "avav"
-LAST = "vavavava"
-PEV = "vaa"
-XG = "aaa"
-XEV = "aaaaa"
-QF = "v"
-ORDER = ["""place0 list0 place1 x0 fill0 ghostE send later turn0 xt0 fill2 tell fill1 q0 old2 diff2 list1 x1 turn1 xt1 cmp2 qf0 old0 sum0 fill3 q4 qf4
-old4 cmp0 latest val0 count0.0 sum2 turn2 count0.1 aim0 put0 q8 diff4 val2 xt2 old8 cmp4 count2.0 count2.1 put1 sum4 val4 aim2 put2 count4.0 turn3
-count4.1 diff8 qf8 put3 q12 old12 aim4 xt3 cmp8 count8.0 sum8 val8 diff12 cmp12 count8.1 qf12 put4 heard put5 q16 put6 put7 old16 aim8 put8 put9 put10
-turn4 xt4 count12.0 sum12 val12 count12.1 aim12 diff16 cmp16 put11 qf16 sum16 val16 count16.0 count16.1 marks0 put12 put13 put14 aim16 marks1.0 marks1.4
-marks1.8 marks1.12 keep1 put15 put16 put17 put18 keep0""",
-         """copy4 copy0 copy2 copy1 copy3 marks0 keep0 runs0 marks1.0 marks1.4 marks1.8 marks1.12 keep1 cum0 le0 run0 empty0 place0.0 runlist0 rank0 runs1
-within0 place0.2 cum1 le1 rank1 run1 empty1 list0 x0 place1.0 send runlist1 tell q0 turn0 within1 place1.2 old0 list1 q4 old2 xt0 sum0 x1 qf0 old4 cmp0
-val0 qf4 sum2 count0.0 turn1 xt1 count0.1 diff2 val2 cmp2 aim0 diff4 put0 put1 old8 cmp4 count2.0 count2.1 aim2 put2 turn2 xt2 sum4 val4 put3 count4.0
-count4.1 aim4 put4 put5 diff8 old12 cmp8 sum8 turn3 xt3 count8.0 count8.1 heard put6 q16 val8 old16 put7 aim8 put8 qf16 diff12 cmp12 sum12 turn4 xt4
-count12.0 count12.1 diff16 val12 cmp16 sum16 val16 put9 put10 put11 aim12 put12 count16.0 count16.1 put13 put14 aim16 put15 put16 put17 put18"""]
+COPY = [(0, 1344, "s"), (1344, 2688, "s"), (2688, V, "g")]
+FILL = "vvvv"
+XQ = "aa" * 8
+CUT = 512
+TELL = "gg"
+KEEP = "a"
+QF = "g"
+ORDER = ["""place0 list0 fill0 q0 x2 x0 turn0 xt0 old0 turn2 xt2 sum0 qf0 send tell fill1 fill3 q2 old2 others qf2 diff2 x4 cmp2 cmp0 turn4 count0 fill2 val0 spare1 q4 xt4 old4 spare0 aim0 spare4 spare2 sum2 count2 spare3 spare5 qf4 turn8 xt8 diff4 put0 spare6 q8 later qf8 put1 val2 aim2 put2 q12 put3 sum4 old8 diff8 cmp4 val4 old12 turn12 xt12 count4 aim4 qf12 ghostE sum8 cmp8 diff12 val8 put4 put5 count8 turn16 sum12 jump put6 put7 heard aim8 q16 put8 qf16 put9 put10 cmp12 latest count12 old16 xt16 diff16 val12 cmp16 aim12 put11 put12 put13 put14 sum16 val16 count16 marks1.0 marks1.4 marks1.8 marks1.12 keep1 aim16 put15 put16 put17 put18""",
+         """stale3 stale2 stale1 copy1 stale0 copy0 fresh0 fresh3 fresh1 fresh2 marks1.0 scan0 scan1 tally0 scan2 tally1 scan3 lu0 tally2 lu1 lx0 q0 lx1 tally3 lu3 marks1.4 marks1.8 marks1.12 keep1 runs1 x0 old0 lu2 lx3 q2 lx2 cum1 le1 rank1 run1 empty1 runlist1 turn0 xt0 x2 sum0 turn2 old2 place1.0 within1 qf0 copy2 send qf2 tell xt2 place1.2 cmp0 diff2 count0 list1 q4 val0 x4 qf4 cmp2 old4 aim0 put0 turn4 sum2 val2 xt4 count2 turn8 diff4 old8 sum4 aim2 put1 put2 put3 cmp4 xt8 count4 aim4 diff8 val4 put4 put5 old12 cmp8 sum8 turn12 xt12 count8 val8 heard put6 q16 old16 put7 aim8 qf16 turn16 diff12 cmp12 xt16 sum12 val12 count12 diff16 cmp16 sum16 val16 put8 put9 put10 put11 aim12 count16 put12 put13 put14 put15 aim16 put16 put17 put18"""]
 
 SCRATCH = {}
-for _n, _w, _d in (("fr_s", 16, "int32"), ("rb", W0, "bfloat16"), ("wn", 2 * W0, "float32"), ("up_s", UP, "int32"),
+for _n, _w, _d in (("fr_s", 16, "int32"), ("w0", OFF + W0, "bfloat16"), ("w1", OFF + W0, "bfloat16"), ("up_s", UP, "int32"),
                    ("kI", 8, "int32"), ("kc", 8, "float32"), ("E", 1024, "bfloat16"), ("EG", 768, "bfloat16"), ("ID", 128, "bfloat16"),
-                   ("HI", 128, "bfloat16"), ("NI", 128, "bfloat16"), ("HF", 128, "float32"), ("I64", 128, "float32"), ("I16", 128, "bfloat16"),
-                   ("WS", 144, "bfloat16"), ("W2", 144, "bfloat16"), ("WM", 144, "bfloat16"), ("AP", 128, "bfloat16"), ("AN", 128, "bfloat16"),
-                   ("LP", 128, "bfloat16"), ("LN", 128, "bfloat16"), ("MK", B, "bfloat16"), ("CB", B, "bfloat16"), ("KC", 256, "bfloat16"),
-                   ("TJ", 16, "float32"), ("J", 16, "float32"), ("TB", 16, "float32"), ("XT", 128 * 5, "bfloat16"),
+                   ("HI", 128, "bfloat16"), ("NI", 128, "bfloat16"), ("HF", 128, "float32"), ("IF", 128, "float32"), ("I16", 128, "bfloat16"),
+                   ("WS", 144, "bfloat16"), ("W1", 144, "bfloat16"), ("W2", 144, "bfloat16"), ("WM", 144, "bfloat16"), ("AP", 128, "bfloat16"),
+                   ("AN", 128, "bfloat16"), ("LP", 128, "bfloat16"), ("LN", 128, "bfloat16"), ("MK", B, "bfloat16"), ("CB", B, "bfloat16"),
+                   ("KC", 256, "bfloat16"), ("KR", 128 * len(ROWS), "bfloat16"),
+                   ("TJ", 16, "float32"), ("J", 16, "float32"), ("TB", 24, "float32"), ("XT", 128 * 8, "bfloat16"), ("BP", 128, "bfloat16"),
+                   ("BN", 128, "bfloat16"), ("ON", S, "bfloat16"), ("ST", S, "bfloat16"), ("r1", 6 * S, "bfloat16"), ("junk", 6 * S, "bfloat16"),
+                   ("sums", 8, "float32"), ("lx", 8, "uint16"), ("dm", 16, "int32"),
                    ("m0", B, "bfloat16"), ("m1", B, "bfloat16"), ("cum", B, "bfloat16"), ("le", B, "bfloat16"), ("hi", B, "bfloat16"),
-                   ("rk", B, "bfloat16"), ("i16", 16, "uint16"), ("c2", 256, "bfloat16"), ("ej", 16, "float32"), ("tu", 16, "float32"),
+                   ("rk", B, "bfloat16"), ("i16", 16, "uint16"), ("c2", 256, "bfloat16"), ("ej", 16, "float32"), ("tu", 24, "float32"),
                    ("lu", 32, "uint16"), ("q16", 16 * NB, "uint16"), ("qf", 16 * NB, "float32"), ("x", 16 * NO, "bfloat16"),
-                   ("old", 256 * NB, "bfloat16"), ("cb", 256 * NB, "bfloat16"), ("val", 256 * NB, "float32"), ("o16", 16 * NB, "uint16")):
+                   ("old", 256 * NB, "bfloat16"), ("cb", 256 * NB, "bfloat16"), ("val", 256 * NB, "bfloat16"), ("o16", 16 * NB, "uint16")):
     SCRATCH[_n] = ("sbuf", [128, _w], _d)
 for _i in range(WAVES):
     SCRATCH["snd%d" % _i] = ("sbuf", [128, D * PW], "float32")
@@ -49,7 +50,7 @@ for _i in range(WAVES):
 PSUM = {"p0": 1024, "p1": 1024, "p2": 1024, "px": 512, "pc": 512}
 for _n in PSUM:
     SCRATCH[_n] = ("psum", [128, PSUM[_n]], "float32")
-SEMAPHORES = ["sv", "sa", "sp", "sg", "sent"] + ["gh%d" % i for i in range(WAVES)] + ["d%d" % i for i in range(24)]
+SEMAPHORES = ["sv", "sa", "sp", "sg", "sent"] + ["gh%d" % i for i in range(WAVES)] + ["d%d" % i for i in range(32)]
 
 COST = {"cyc": 1e-3, "ga": 1.5, "sc": 3.0, "pe": 0.5e-3, "mm": 0.02, "hop": 0.12, "lat": 5.0, "call": 1.5, "bw": 200e3, "dlat": 1.8, "eps": 0.1}
 
@@ -93,16 +94,16 @@ def plan():
         if psum:
             lo, hi = lo // 512 * 512, -(-hi // 512) * 512
         keep = []
-        for (l, h, j, k) in hist.get(buf, []):
-            if j != i and l < hi and lo < h and (psum or kind == "w" or k == "w"):
+        for (l, h, j, k, p0, p1) in hist.get(buf, []):
+            if j != i and l < hi and lo < h and (psum or (p0 < r[5] and r[4] < p1 and "w" in (k, kind))):
                 a, b = ops[j], ops[i]
                 if a["q"] == "p" and b["q"] == "p":
                     deps.setdefault(j, False)
                 else:
-                    deps[j] = deps.get(j, False) or k == "w" or a["dma"] > 0 or b["dma"] > 0 or a["q"] != b["q"]
-            if not (lo <= l and h <= hi and kind == "w" and j != i and r[3] == 1):
-                keep.append((l, h, j, k))
-        hist[buf] = keep + [(lo, hi, i, kind)]
+                    deps[j] = deps.get(j, False) or "w" in (k, kind) or a["dma"] > 0 or b["dma"] > 0 or a["q"] != b["q"]
+            if not (lo <= l and h <= hi and kind == "w" and j != i and (psum or (r[3] == 1 and r[4] <= p0 and p1 <= r[5]))):
+                keep.append((l, h, j, k, p0, p1))
+        hist[buf] = keep + [(lo, hi, i, kind, r[4], r[5])]
 
     def add(q, fn, reads, writes, cost, dma=0, lat=0.0):
         ops.append({"q": q, "fn": fn, "cost": cost, "dma": dma, "lat": lat, "deps": {}, "at": tuple(now)})
@@ -125,13 +126,19 @@ def plan():
         add("v", lambda g, T: g.vector.memset(ap(T, r), x), [], [r], cy(r, r, 0.5))
 
     def copy(q, out, in_, bias=0.0):
+        n = width(out)
         if q == "v":
             add("v", lambda g, T: g.vector.tensor_copy(ap(T, out), ap(T, in_)), [in_], [out], cy(out, in_, half(out, in_)))
         elif q == "a":
             add("a", lambda g, T: g.scalar.activation(ap(T, out), ap(T, in_), ACT.Copy, bias=bias), [in_], [out], cy(out, in_))
-        else:
-            n = width(out)
+        elif q == "g":
             add("g", lambda g, T: g.affine_select(ap(T, out), ap(T, in_), [[0, n]], OP.is_equal, 0.0, 0, 0), [in_], [out], 0.17 + 2 * C["cyc"] * n)
+        else:
+            add("s", lambda g, T: g.sync.dma_start(ap(T, out), ap(T, in_)), [in_], [out], 0.06, 256 * n)
+
+    def times(out, in_, by):
+        col = [R("kc", by, by + 1)] if isinstance(by, int) else []
+        add("a", lambda g, T: g.scalar.activation(ap(T, out), ap(T, in_), ACT.Copy, scale=ap(T, col[0]) if col else by), [in_] + col, [out], cy(out, in_))
 
     def scal(out, in_, a, b, o0, o1=None):
         reads, more = [in_] + ([a] if isinstance(a, tuple) else []), ([] if o1 is None else [o1])
@@ -144,20 +151,25 @@ def plan():
     def scan(out, x, y, o0, o1):
         add("v", lambda g, T: g.vector.tensor_tensor_scan(ap(T, out), ap(T, x), ap(T, y), 0.0, o0, o1), [x, y], [out], cy(out, y, half(out, y)))
 
-    def sign(out, in_):
-        add("a", lambda g, T: g.scalar.activation(ap(T, out), ap(T, in_), ACT.Sign, bias=0.0, scale=-1.0), [in_], [out], cy(out, in_))
+    def sign(out, in_, bias=None, acc=None):
+        add("a", lambda g, T: g.scalar.activation(ap(T, out), ap(T, in_), ACT.Sign, bias=ap(T, bias) if bias else 0.0, scale=-1.0,
+                                                  accum_out=ap(T, acc) if acc else None), [in_] + [bias] * bool(bias), [out] + [acc] * bool(acc),
+            cy(out, in_) + 0.02 * bool(acc))
 
-    def mm(*terms, cut=()):
+    def mm(*terms, cut=(), onto=False, last=True):
         name = now[1]
         for lo, hi in zip((0,) + cut, cut + (len(terms),)):
             def fn(g, T, lo=lo, hi=hi):
                 for i in range(lo, hi):
-                    r = g.tensor.matmul(*[ap(T, z) for z in terms[i]], i == 0, i == len(terms) - 1)
+                    r = g.tensor.matmul(*[ap(T, z) for z in terms[i]], i == 0 and not onto, last and i == len(terms) - 1)
                 return r
             cost = sum(C["mm"] + max(64, width(t[2])) * C["pe"] * (1 if narrow(t[2]) else 4) for t in terms[lo:hi])
             step(name, "." + str(lo) if cut else "")
             add("p", fn, [r for t in terms[lo:hi] for r in t[1:]], [terms[0][0]], cost)
         step(name)
+
+    def plus(o, i):
+        return (o, R("KR", 128 * i, 128 * i + 128, 1, 64, 65), R("E", 0, width(o), 1, 64, 65))
 
     def pick(r, pat, op, x, base, cm):
         add("g", lambda g, T: g.affine_select(ap(T, r), ap(T, r), pat, op, x, base, cm), [r], [r], 0.17 + 2 * C["cyc"] * width(r))
@@ -165,70 +177,103 @@ def plan():
     def iota(r, pat, base, cm):
         add("g", lambda g, T: g.iota(ap(T, r), pat, base, cm, allow_small_or_imprecise_dtypes=True), [], [r], 0.13 + 2 * C["cyc"] * width(r))
 
-    def nodes(lo, hi):
-        return R("wn", 2 * lo + 1, 2 * hi, 2)
-
     load("s", R("fr_s", 0, 16), "fr", 0, 16, 8192)
-    load("a", R("up_s", 0, 4 * B), "up", 0, 4 * B, 2048 * B)
-    for j in range(4):
-        load("s", R("rb", j * V // 4, (j + 1) * V // 4), "rec", j * V // 4, (j + 1) * V // 4, 64 * V)
-    for b in range(4, NO, 4):
-        load("s", R("up_s", b * B, (b + 4) * B), "up", b * B, (b + 4) * B, 2048 * B)
-    load("s", R("up_s", GH, GH + D * B), "up", V, V + D * B, 512 * D * B)
+    for b in range(2):
+        load("a", R("up_s", b * S, b * S + B), "up", b * B, b * B + B, 512 * B)
+    for lo, hi in ((0, V // 4), (V // 4, V)):
+        load("s", R("w0", lo, hi), "rec", lo, hi, 256 * (hi - lo))
+    for b in range(2, F):
+        load("s", R("up_s", b * S, b * S + B), "up", b * B, b * B + B, 512 * B)
+    for b0, b1 in [u[:2] for u in UNITS if F <= u[0] < NO]:
+        load("s", R("up_s", M0 + b0 * B, M0 + b1 * B), "up", b0 * B, b1 * B, 512 * B * (b1 - b0))
+    for d in range(D):
+        load("s", R("up_s", GH + d * S, GH + d * S + B), "up", V + d * B, V + d * B + B, 512 * B)
 
     whole = lambda n: R(n, 0, SCRATCH[n][1][1])
-    for n, x in (("ID", 1.0), ("E", 1.0), ("AP", 1.0), ("EG", 1.0), ("WS", 0.0), ("WM", 0.0), ("MK", 1.0), ("XT", -0.25)):
+    nx = 128 * len(UNITS)
+    for n, x in (("ID", 1.0), ("AP", 1.0), ("E", 1.0), ("WS", 0.0), ("WM", 0.0), ("EG", 1.0)):
         fill(whole(n), x)
-    fill(R("rb", V, W0), 0.0)
-    iota(whole("TB"), [[B, NO]], 0, 0)
     iota(R("kI", 0, 1), [[0, 1]], 0, 1)
     pick(whole("ID"), [[-1, 128]], OP.is_equal, 0.0, 0, 1)
+    iota(R("TB", 0, F), [[S, F]], 0, 0)
+    iota(R("TB", F, NO), [[B, NO - F]], F * B, 0)
+    iota(R("TB", NO, NO + F), [[B, F]], 0, 0)
+    iota(whole("dm"), [[16, 16]], V, 1)
     pick(whole("AP"), [[-16, 8], [0, 16]], OP.is_ge, 0.0, 0, 1)
     pick(whole("AP"), [[16, 8], [0, 16]], OP.is_ge, 0.0, 15, -1)
     pick(R("E", 0, 1024, 1, 0, 64), [[1, 64], [0, 16]], OP.is_equal, 0.0, 0, -1)
-    iota(R("up_s", UP - 16, UP), [[16, 16]], V, 1)
-    fill(R("XT", 15, 640, 16), 1.0)
-    fill(R("MK", 0, B, BL), 0.0)
+    fill(R("XT", 0, nx, 1, 64, 96), -0.25)
+    fill(R("XT", 0, nx, 1, 0, 64), 0.0)
     scal(R("kI", 1, 2), R("kI", 0, 1), 15, None, OP.bitwise_and)
-    fill(R("XT", 0, 640, 1, 0, 64), 0.0)
-    scal(whole("HI"), whole("ID"), 0.5, None, OP.mult)
+    fill(R("XT", 15, nx, 16, 64, 96), 1.0)
+    fill(R("w0", V, W0), 0.0)
     copy("v", R("kc", 0, 1), R("kI", 1, 2))
-    scal(R("kc", 1, 2), R("kI", 1, 2), float(D * B), None, OP.add)
-    fill(R("HI", 15, 128, 16), 0.0)
-    scal(whole("I64"), whole("ID"), 64.0, None, OP.mult)
-    scal(whole("I16"), whole("ID"), 16.0, None, OP.mult)
-    scal(whole("NI"), whole("HI"), -1.0, None, OP.mult)
-    copy("v", whole("HF"), whole("HI"))
-    copy("v", R("WM", 15, 128, 16), R("ID", 15, 128, 16))
-    copy("v", R("WS", 15, 128, 16), R("AP", 15, 128, 16))
-    scal(whole("AN"), whole("AP"), -1.0, None, OP.mult)
-    copy("v", whole("LP"), whole("AP"))
-    scal(whole("W2"), whole("WS"), 2.0, None, OP.mult)
+    scal(R("kc", 1, 2), R("kI", 1, 2), 0.5, None, OP.add)
+    scal(R("kc", 2, 3), R("kI", 1, 2), 15.0, None, OP.is_equal)
+    for at in [b * S + B for b in range(F)]:
+        copy("v", R("up_s", at, at + 16), whole("dm"))
+    for i, (note, mark) in enumerate(((0.5, 0.0), (-0.5, 0.0), (-128.0, -2304.0), (256.0, 384.0), (0.0, -1.0))):
+        scal(R("kc", 3 + i, 4 + i), R("kc", 2, 3), mark - note, note, OP.mult, OP.add)
+    for i, x in enumerate(ROWS):
+        fill(R("KR", 128 * i, 128 * i + 128), x)
+    copy("a", whole("IF"), whole("ID"))
+    copy("a", R("WM", 15, 128, 16), R("ID", 15, 128, 16))
+    copy("a", R("WS", 15, 128, 16), R("AP", 15, 128, 16))
+    copy("a", whole("LP"), whole("AP"))
+    for out, in_, by in (("HI", "ID", 3), ("NI", "ID", 4), ("HF", "ID", 3), ("W1", "WS", 5), ("W2", "WS", 6), ("BP", "AP", 2), ("BN", "AP", 7),
+                         ("I16", "ID", 16.0), ("AN", "AP", -1.0)):
+        times(whole(out), whole(in_), by)
+    for i, (r, x) in enumerate(((whole("MK"), 1.0), (whole("ON"), 1.0), (whole("rk"), 0.0), (R("w1", V, W0), 0.0), (R("ST", 0, B), 0.0),
+                                (R("ST", B, S), 1.0), (R("MK", 0, B, BL), 0.0))):
+        step("spare", i)
+        fill(r, x)
+    step("others")
+    for at in [M0 + V] + [GH + d * S + B for d in range(D)]:
+        copy("g", R("up_s", at, at + 16), whole("dm"))
     step("ghostE")
     pick(R("EG", 0, 768, 1, 0, 64), [[PW, D], [1, 16], [0, 16]], OP.is_equal, 0.0, 0, -1)
     step("later")
-    iota(R("up_s", V, GH), [[16, 16]], V, 1)
     pick(whole("LP"), [[-1, 128]], OP.is_gt, 0.0, 0, 1)
     iota(whole("CB"), [[BL, NO], [0, BL]], 0, 0)
     iota(whole("KC"), [[0, NO], [1, 16]], 0, 0)
     iota(whole("TJ"), [[-B, NO]], V - B, 0)
     step("latest")
-    scal(whole("LN"), whole("LP"), -1.0, None, OP.mult)
-    scal(whole("J"), whole("TJ"), R("kc", 0, 1), 1.0 / 64, OP.add, OP.mult)
+    times(whole("LN"), whole("LP"), -1.0)
+    step("jump")
+    scal(whole("J"), whole("TJ"), R("kc", 0, 1), None, OP.add)
     for j in range(4):
         step("fill", j)
-        copy(FILL[j], nodes(j * V // 4, (j + 1) * V // 4), R("rb", j * V // 4, (j + 1) * V // 4))
+        copy(FILL[j], R("w1", j * V // 4, (j + 1) * V // 4), R("w0", j * V // 4, (j + 1) * V // 4))
 
-    def marks(w, gi):
-        b0, b1, t = GROUPS[gi][:3]
+    def marks(w, gi=1):
+        b0, b1, t = F, NO, "p2"
         o = R(t, 0, BL * (b1 - b0))
         step("marks", gi)
-        mm(*[(o, R("WM", 15 - j, 143 - j), R("rb", b0 * B + j, b1 * B, 16)) for j in range(16)], cut=(4, 8, 12) if gi else ())
+        mm(*[(o, R("WM", 15 - j, 143 - j), R("w%d" % (w % 2), b0 * B + j, b1 * B, 16)) for j in range(16)], cut=(4, 8, 12))
         step("keep", gi)
-        copy(PEV[gi], R("m%d" % (w % 2), b0 * BL, b1 * BL), o)
+        copy(KEEP, R("m%d" % (w % 2), b0 * BL, b1 * BL), o)
 
-    def frontier(w, gi):
-        b0, b1, t, t2, at = GROUPS[gi]
+    def before(w, b):
+        t, at = FRESH[b]
+        step("stale", b)
+        mm((R(t, at, at + S), R("E", 0, 128, 1, 64, 65), R("ST", 0, S, 1, 64, 65)),
+           (R(t, at, at + B), whole("BN"), R("w%d" % ((w + 1) % 2), b * B, b * B + B)), last=False)
+
+    def first(w, b):
+        t, at = FRESH[b]
+        step("fresh", b)
+        mm((R(t, at, at + B), whole("BP"), R("w%d" % (w % 2), b * B, b * B + B)), onto=True)
+        step("scan", b)
+        scan(R("r1", b * S, b * S + S), whole("ON"), R(t, at, at + S), OP.mult, OP.add)
+        step("tally", b)
+        sign(R("junk", b * S, b * S + S), R("r1", b * S, b * S + S), R("kc", 1, 2), R("sums", b, b + 1))
+        step("lu", b)
+        scal(R("lu", b, b + 1), R("sums", b, b + 1), 0.5, float(S // 2 + S * b), OP.mult, OP.add)
+        step("lx", b)
+        scal(R("lx", b, b + 1), R("sums", b, b + 1), 0.5, float(S // 2 + B * b), OP.mult, OP.add)
+
+    def frontier(w, gi=1):
+        b0, b1, t, t2, at = F, NO, "p2", "p2", 512
         lo, hi, n = b0 * BL, b1 * BL, BL * (b1 - b0)
         new, was = R("m%d" % (w % 2), lo, hi), R("m%d" % ((w - 1) % 2), lo, hi)
         tot, rest = R(t2, at, at + n), R(t2, at + 256, at + 256 + n)
@@ -252,12 +297,13 @@ def plan():
         both(R("c2", b0 * 16, b1 * 16), ("at", R("rk", 0, hi), R("i16", b0, b1)), R("KC", b0 * 16, b1 * 16), OP.is_le)
         o = R(t, 0, b1 - b0)
         step("place", gi)
-        mm(*([(o, whole("I16"), run), (o, whole("I64"), R("ej", b0, b1))]
+        mm(*([(o, whole("I16"), run), (o, whole("IF"), R("ej", b0, b1))]
              + [(o, R("WS", 15 - k, 143 - k), R("c2", b0 * 16 + k, b1 * 16, 16)) for k in range(16)]), cut=(2,))
         return o
 
     def wave(w):
-        src, snd, rcv = whole("rb"), "snd%d" % w, "rcv%d" % w
+        was, new, snd, rcv = "w%d" % (w % 2), "w%d" % ((w + 1) % 2), "snd%d" % w, "rcv%d" % w
+        src = R(was, 0, W0)
         now[0] = w
 
         def parents(lo, hi, win):
@@ -267,96 +313,111 @@ def plan():
             step("qf", lo)
             copy(QF, R("qf", lo * 16, hi * 16), q)
 
-        def turn(k, m, buf, lo, by):
-            step("turn", k)
-            mm((R("px", 0, 128, 1, 0, m), R(buf, lo, lo + m), whole(by)))
-            step("xt", k)
-            copy(XEV[k], R("XT", k * 128, k * 128 + 128, 1, 0, m), R("px", 0, 128, 1, 0, m))
-
-        def unit(b0, b1, qs, pd, ps):
-            k, lo, hi, n = b0 // 4, b0 * 256, b1 * 256, 16 * (b1 - b0)
+        def unit(k):
+            b0, b1, qs, pd, ps = UNITS[k]
+            lo, hi, n = b0 * 256, b1 * 256, 16 * (b1 - b0)
             l16, h16, m = b0 * 16, b1 * 16, hi - lo
+            rows, notes, by = (n, R("x", l16, h16), "HI") if b0 < NO else ((b1 - b0) * PW, R(rcv, (b0 - NO) * PW, (b1 - NO) * PW), "HF")
+            step("turn", b0)
+            mm((R("px", 0, 128, 1, 0, rows), notes, whole(by)))
+            step("xt", b0)
+            copy(XQ[2 * k + 1], R("XT", k * 128, k * 128 + 128, 1, 0, rows), R("px", 0, 128, 1, 0, rows))
             od = R("old", lo, hi)
             step("old", b0)
             copy(qs[0], od, ("at", src, R("q16", l16, h16)))
 
-            def spread(t, at, by):
+            def spread(t, at, by, rounds):
                 for a in range(0, m, 512):
-                    z, eo = min(a + 512, m), (b0 % 4) * 256
+                    z = min(a + 512, m)
                     o = R(t, at + a, at + z)
-                    mm((o, R("XT", k * 128, k * 128 + 128, 1, 0, 65), R("EG" if b0 == NO else "E", eo + a, eo + z, 1, 0, 65)), (o, whole(by), R("old", lo + a, lo + z)))
+                    mm(*([(o, R("XT", k * 128, k * 128 + 128, 1, 0, 65), R("EG" if b0 >= NO else "E", a, z, 1, 0, 65)),
+                          (o, whole(by), R("old", lo + a, lo + z))] + [plus(o, 0)] * rounds))
                 return R(t, at, at + m)
             if qs[1] == "a":
                 step("diff", b0)
-                s = spread(*pd, "NI")
+                s = spread(*pd, "NI", False)
                 step("cmp", b0)
                 sign(R("cb", lo, hi), s)
             step("sum", b0)
-            s = spread(*ps, "HI")
+            s = spread(*ps, "HI", qs[2] == "a")
             if qs[1] == "v":
-                step("cmp", b0)
-                both(R("cb", lo, hi), od, s, OP.is_gt, 1.0)
+                for a in range(0, m, CUT):
+                    step("cmp", b0 + a // 256)
+                    z = min(a + CUT, m)
+                    both(R("cb", lo + a, lo + z), R("old", lo + a, lo + z), R(s[0], s[1] + a, s[1] + z), OP.is_le, 1.0)
             step("val", b0)
             if qs[2] == "a":
-                copy("a", R("val", lo, hi), s, BIG)
+                copy("a", R("val", lo, hi), s, -BIG)
             else:
-                scal(R("val", lo, hi), s, BIG, None, OP.add)
+                for a in range(0, m, CUT):
+                    step("val", b0 + a // 256)
+                    z = min(a + CUT, m)
+                    scal(R("val", lo + a, lo + z), R(s[0], s[1] + a, s[1] + z), BIG, BIG, OP.add, OP.subtract)
             o = R("pc", 0, n)
             step("count", b0)
-            mm(*([(o, whole("I64"), R("qf", l16, h16))] + [(o, R("WS" if qs[1] == "a" else "W2", 15 - i, 143 - i), R("cb", lo + i, hi, 16)) for i in range(16)]), cut=(1,))
+            mm(*([(o, R("W1" if qs[1] == "a" else "W2", 15 - i, 143 - i), R("cb", lo + i, hi, 16)) for i in range(16)]
+                 + [plus(o, 1), plus(o, 2), (o, whole("IF"), R("qf", l16, h16))]))
             step("aim", b0)
-            scal(R("o16", l16, h16), o, 1.0 / 32, (15.0 if qs[1] == "a" else -1.0) / 32, OP.mult, OP.add)
+            copy("v", R("o16", l16, h16), o)
             for b in range(b0, b1):
                 step("put", b)
-                scal(("at", whole("wn"), R("o16", b * 16, b * 16 + 16)), R("val", b * 256, b * 256 + 256), 1.0, -BIG, OP.mult, OP.add)
+                copy("v", ("at", whole(new), R("o16", b * 16, b * 16 + 16)), R("val", b * 256, b * 256 + 256))
 
-        for j, (lo, hi, q) in enumerate(COPY if w else []):
-            step("copy", j)
-            copy(q, R("rb", lo, hi), nodes(lo, hi))
-        for gi, (b0, b1, _, _, _) in enumerate(GROUPS):
-            if w == 0:
-                node = R("tu", b0, b1)
-                step("place", gi)
-                both(node, R("fr_s", b0, b1), R("TB", b0, b1), OP.add)
-            else:
-                marks(w, gi)
-                node = frontier(w, gi)
-            step("list", gi)
-            copy("v", R("lu", b0, b1), node)
-            for b in range(b0, b1, 4 if w == 0 else NO):
-                z = min(b + 4, b1) if w == 0 else b1
-                parents(b, z, R("up_s", 0, GH if w else z * B))
-            step("x", gi)
-            copy(XG[gi], R("x", b0 * 16, b1 * 16), ("at", src if w else R("rb", 0, b1 * B), R("lu", b0, b1)))
-            if b0 == 0:
-                step("tell")
-                scal(R(snd, 16, D * PW, PW), R(node[0], node[1], node[1] + D), R("kc", 1, 2), None, OP.min)
-                step("send")
-                for d in range(D):
-                    copy("g", R(snd, d * PW, d * PW + 16), R("x", d * 16, d * 16 + 16))
-                add("g", w, [whole(snd)], [whole(rcv)], C["call"], 0, C["lat"])
-            for u in UNITS:
-                if b0 <= u[0] < b1:
-                    if u[0] % 4 == 0:
-                        turn(u[0] // 4, 64, "x", u[0] * 16, "HI")
-                    unit(*u)
-        step("heard")
-        copy("v", R("lu", NO, NB), R(rcv, 16, D * PW, PW))
-        parents(NO, NB, R("up_s", GH, UP))
-        turn(4, D * PW, rcv, 0, "HF")
-        unit(*UNITS[-1])
         if w == 0:
-            for gi in range(len(GROUPS)):
-                marks(0, gi)
+            step("place", 0)
+            both(R("tu", 0, NO), whole("fr_s"), R("TB", 0, NO), OP.add)
+            both(R("tu", NO, NO + F), R("fr_s", 0, F), R("TB", NO, NO + F), OP.add)
+            step("list", 0)
+            copy("v", R("lu", 0, NO), R("tu", 0, NO))
+            copy("v", R("lx", 0, F), R("tu", NO, NO + F))
+        else:
+            for b in range(F):
+                before(w, b)
+            for j, (lo, hi, q) in enumerate(COPY):
+                step("copy", j)
+                copy(q, R(new, lo, hi), R(was, lo, hi))
+            for b in range(F):
+                first(w, b)
+        early = [k for k, u in enumerate(UNITS) if u[0] < F]
+        for k in early:
+            b0, b1 = UNITS[k][:2]
+            parents(b0, b1, R("up_s", 0, b1 * S))
+            step("x", b0)
+            copy(XQ[2 * k], R("x", b0 * 16, b1 * 16), ("at", R(was, 0, b1 * B + 16 * (w > 0)), R("lx", b0, b1)))
+        step("tell")
+        copy(TELL[0], R(snd, 16, D * PW, PW), R("lu", 0, D))
+        step("send")
+        for d in range(D):
+            copy("g", R(snd, d * PW, d * PW + 16), R("x", d * 16, d * 16 + 16))
+        add("g", w, [whole(snd)], [whole(rcv)], C["call"], 0, C["lat"] + 4.0 * (w == 0))
+        if w:
+            marks(w)
+            node = frontier(w)
+        for k in early:
+            unit(k)
+        if w:
+            step("list", 1)
+            copy("v", R("lu", F, NO), node)
+        for b0, b1 in [(F, NO)] if w else [u[:2] for u in UNITS if F <= u[0] < NO]:
+            parents(b0, b1, R("up_s", M0, GH if w else M0 + b1 * B))
+        step("x", F)
+        copy(XQ[2 * len(early)], R("x", F * 16, NO * 16), ("at", src, R("lu", F, NO)))
+        for k in [k for k, u in enumerate(UNITS) if F <= u[0] < NO]:
+            unit(k)
+        step("heard")
+        copy(TELL[1], R("lu", NO, NB), R(rcv, 16, D * PW, PW))
+        parents(NO, NB, R("up_s", GH, UP))
+        for k in [k for k, u in enumerate(UNITS) if NO <= u[0]]:
+            unit(k)
+        if w == 0:
+            marks(0)
 
     for w in range(WAVES):
         wave(w)
     now[0] = WAVES
-    for j, q in enumerate(LAST):
-        lo, hi = j * V // len(LAST), (j + 1) * V // len(LAST)
-        o = R("rb", lo, hi)
-        copy(q, o, nodes(lo, hi))
-        add("s", lambda g, T, o=o: g.sync.dma_start(T.y[:, o[1]:o[2]], ap(T, o)), [o], [], 0.06, 256 * (hi - lo))
+    for j, q in enumerate("sa"):
+        o = R("w%d" % (WAVES % 2), j * V // 2, (j + 1) * V // 2)
+        add(q, lambda g, T, o=o, q=q: (g.sync if q == "s" else g.scalar).dma_start(T.y[:, o[1]:o[2]], ap(T, o)), [o], [], 0.06, 128 * V)
     return ops
 
 

from concourse.bass import DstId, RemoteDMATransfer
from concourse.mybir import AluOpType, ActivationFunctionType

OP, ACT = AluOpType, ActivationFunctionType
N, B, NO, NB, D, WAVES = 4, 224, 16, 19, 3, 4
V = NO * B
W0 = V + 384
OFF = 4096
S = B + 16
F = 4
M0 = 16 * F
GH = M0 + V + 16
UP = GH + D * S
BL = B // 16
PW = 17
BIG = 2.0 ** 23
HUGE = BIG * OFF
ROWS = [BIG, HUGE, -HUGE]
FRESH = [("p0", 0), ("p0", 512), ("p1", 0), ("p1", 512), ("px", 0), ("pc", 0)]
UNITS = [(0, 2, "avv", None, ("p0", 0)), (2, 4, "aav", ("p1", 0), ("p1", 512)), (4, 8, "aaa", ("p2", 0), ("p0", 0)),
         (8, 12, "aaa", ("p1", 0), ("p2", 0)), (12, 16, "aaa", ("p0", 0), ("p1", 0)), (16, 19, "aaa", ("p2", 0), ("p0", 0))]
COPY = [(0, 1344, "s"), (1344, 2688, "s"), (2688, V, "g")]
FILL = "vvvv"
XQ = "aa" * 8
CUT = 512
TELL = "gg"
KEEP = "a"
QF = "g"
ORDER = ["""place0 list0 fill0 q0 x2 x0 turn0 xt0 old0 turn2 xt2 sum0 qf0 send tell fill1 fill3 q2 old2 others qf2 diff2 x4 cmp2 cmp0 turn4 count0 fill2 val0 spare1 q4 xt4 old4 spare0 aim0 spare4 spare2 sum2 count2 spare3 spare5 qf4 turn8 xt8 diff4 put0 spare6 q8 later qf8 put1 val2 aim2 put2 q12 put3 sum4 old8 diff8 cmp4 val4 old12 turn12 xt12 count4 aim4 qf12 ghostE sum8 cmp8 diff12 val8 put4 put5 count8 turn16 sum12 jump put6 put7 heard aim8 q16 put8 qf16 put9 put10 cmp12 latest count12 old16 xt16 diff16 val12 cmp16 aim12 put11 put12 put13 put14 sum16 val16 count16 marks1.0 marks1.4 marks1.8 marks1.12 keep1 aim16 put15 put16 put17 put18""",
         """stale3 stale2 stale1 copy1 stale0 copy0 fresh0 fresh3 fresh1 fresh2 marks1.0 scan0 scan1 tally0 scan2 tally1 scan3 lu0 tally2 lu1 lx0 q0 lx1 tally3 lu3 marks1.4 marks1.8 marks1.12 keep1 runs1 x0 old0 lu2 lx3 q2 lx2 cum1 le1 rank1 run1 empty1 runlist1 turn0 xt0 x2 sum0 turn2 old2 place1.0 within1 qf0 copy2 send qf2 tell xt2 place1.2 cmp0 diff2 count0 list1 q4 val0 x4 qf4 cmp2 old4 aim0 put0 turn4 sum2 val2 xt4 count2 turn8 diff4 old8 sum4 aim2 put1 put2 put3 cmp4 xt8 count4 aim4 diff8 val4 put4 put5 old12 cmp8 sum8 turn12 xt12 count8 val8 heard put6 q16 old16 put7 aim8 qf16 turn16 diff12 cmp12 xt16 sum12 val12 count12 diff16 cmp16 sum16 val16 put8 put9 put10 put11 aim12 count16 put12 put13 put14 put15 aim16 put16 put17 put18"""]

SCRATCH = {}
for _n, _w, _d in (("fr_s", 16, "int32"), ("w0", OFF + W0, "bfloat16"), ("w1", OFF + W0, "bfloat16"), ("up_s", UP, "int32"),
                   ("kI", 8, "int32"), ("kc", 8, "float32"), ("E", 1024, "bfloat16"), ("EG", 768, "bfloat16"), ("ID", 128, "bfloat16"),
                   ("HI", 128, "bfloat16"), ("NI", 128, "bfloat16"), ("HF", 128, "float32"), ("IF", 128, "float32"), ("I16", 128, "bfloat16"),
                   ("WS", 144, "bfloat16"), ("W1", 144, "bfloat16"), ("W2", 144, "bfloat16"), ("WM", 144, "bfloat16"), ("AP", 128, "bfloat16"),
                   ("AN", 128, "bfloat16"), ("LP", 128, "bfloat16"), ("LN", 128, "bfloat16"), ("MK", B, "bfloat16"), ("CB", B, "bfloat16"),
                   ("KC", 256, "bfloat16"), ("KR", 128 * len(ROWS), "bfloat16"),
                   ("TJ", 16, "float32"), ("J", 16, "float32"), ("TB", 24, "float32"), ("XT", 128 * 8, "bfloat16"), ("BP", 128, "bfloat16"),
                   ("BN", 128, "bfloat16"), ("ON", S, "bfloat16"), ("ST", S, "bfloat16"), ("r1", 6 * S, "bfloat16"), ("junk", 6 * S, "bfloat16"),
                   ("sums", 8, "float32"), ("lx", 8, "uint16"), ("dm", 16, "int32"),
                   ("m0", B, "bfloat16"), ("m1", B, "bfloat16"), ("cum", B, "bfloat16"), ("le", B, "bfloat16"), ("hi", B, "bfloat16"),
                   ("rk", B, "bfloat16"), ("i16", 16, "uint16"), ("c2", 256, "bfloat16"), ("ej", 16, "float32"), ("tu", 24, "float32"),
                   ("lu", 32, "uint16"), ("q16", 16 * NB, "uint16"), ("qf", 16 * NB, "float32"), ("x", 16 * NO, "bfloat16"),
                   ("old", 256 * NB, "bfloat16"), ("cb", 256 * NB, "bfloat16"), ("val", 256 * NB, "bfloat16"), ("o16", 16 * NB, "uint16")):
    SCRATCH[_n] = ("sbuf", [128, _w], _d)
for _i in range(WAVES):
    SCRATCH["snd%d" % _i] = ("sbuf", [128, D * PW], "float32")
    SCRATCH["rcv%d" % _i] = ("sbuf", [128, D * PW], "float32")
PSUM = {"p0": 1024, "p1": 1024, "p2": 1024, "px": 512, "pc": 512}
for _n in PSUM:
    SCRATCH[_n] = ("psum", [128, PSUM[_n]], "float32")
SEMAPHORES = ["sv", "sa", "sp", "sg", "sent"] + ["gh%d" % i for i in range(WAVES)] + ["d%d" % i for i in range(32)]

COST = {"cyc": 1e-3, "ga": 1.5, "sc": 3.0, "pe": 0.5e-3, "mm": 0.02, "hop": 0.12, "lat": 5.0, "call": 1.5, "bw": 200e3, "dlat": 1.8, "eps": 0.1}


def R(buf, lo, hi, step=1, p0=0, p1=128):
    return (buf, lo, hi, step, p0, p1)


def ap(T, r):
    if r[0] == "at":
        return ap(T, r[1]).indirect(ap(T, r[2]))
    b, lo, hi, step, p0, p1 = r
    return T[b][p0:p1, lo:hi] if step == 1 else T[b][p0:p1, lo:hi:step]


def width(r):
    return 16 * width(r[2]) if r[0] == "at" else -(-(r[2] - r[1]) // r[3])


def narrow(*rs):
    return all(SCRATCH[r[0]][2] in ("bfloat16", "uint16") for r in rs)


def message(T, U, w, d):
    return T["snd%d" % w][:, d * PW:d * PW + PW], U["rcv%d" % w][:, d * PW:d * PW + PW]


def plan():
    ops, hist, C, now = [], {}, COST, [0, "start"]

    def step(name, i=""):
        now[1] = name + str(i)

    def access(i, r, kind):
        if r[0] == "at":
            access(i, r[1], kind)
            access(i, r[2], "r")
            return
        buf, lo, hi = r[0], r[1], r[2]
        deps, psum = ops[i]["deps"], buf in PSUM
        if psum:
            lo, hi = lo // 512 * 512, -(-hi // 512) * 512
        keep = []
        for (l, h, j, k, p0, p1) in hist.get(buf, []):
            if j != i and l < hi and lo < h and (psum or (p0 < r[5] and r[4] < p1 and "w" in (k, kind))):
                a, b = ops[j], ops[i]
                if a["q"] == "p" and b["q"] == "p":
                    deps.setdefault(j, False)
                else:
                    deps[j] = deps.get(j, False) or "w" in (k, kind) or a["dma"] > 0 or b["dma"] > 0 or a["q"] != b["q"]
            if not (lo <= l and h <= hi and kind == "w" and j != i and (psum or (r[3] == 1 and r[4] <= p0 and p1 <= r[5]))):
                keep.append((l, h, j, k, p0, p1))
        hist[buf] = keep + [(lo, hi, i, kind, r[4], r[5])]

    def add(q, fn, reads, writes, cost, dma=0, lat=0.0):
        ops.append({"q": q, "fn": fn, "cost": cost, "dma": dma, "lat": lat, "deps": {}, "at": tuple(now)})
        for r in reads:
            access(len(ops) - 1, r, "r")
        for r in writes:
            access(len(ops) - 1, r, "w")

    def cy(out, in_, k=1.0):
        k = C["sc"] if out[0] == "at" else (C["ga"] if in_[0] == "at" else k)
        return 0.055 + max(64, width(in_) * k) * C["cyc"]

    def half(out, in_):
        return 0.5 if out[0] != "at" and in_[0] != "at" and narrow(out, in_) else 1.0

    def load(q, out, name, lo, hi, size):
        add(q, lambda g, T: (g.sync if q == "s" else g.scalar).dma_start(ap(T, out), T[name][:, lo:hi]), [], [out], 0.06, size)

    def fill(r, x):
        add("v", lambda g, T: g.vector.memset(ap(T, r), x), [], [r], cy(r, r, 0.5))

    def copy(q, out, in_, bias=0.0):
        n = width(out)
        if q == "v":
            add("v", lambda g, T: g.vector.tensor_copy(ap(T, out), ap(T, in_)), [in_], [out], cy(out, in_, half(out, in_)))
        elif q == "a":
            add("a", lambda g, T: g.scalar.activation(ap(T, out), ap(T, in_), ACT.Copy, bias=bias), [in_], [out], cy(out, in_))
        elif q == "g":
            add("g", lambda g, T: g.affine_select(ap(T, out), ap(T, in_), [[0, n]], OP.is_equal, 0.0, 0, 0), [in_], [out], 0.17 + 2 * C["cyc"] * n)
        else:
            add("s", lambda g, T: g.sync.dma_start(ap(T, out), ap(T, in_)), [in_], [out], 0.06, 256 * n)

    def times(out, in_, by):
        col = [R("kc", by, by + 1)] if isinstance(by, int) else []
        add("a", lambda g, T: g.scalar.activation(ap(T, out), ap(T, in_), ACT.Copy, scale=ap(T, col[0]) if col else by), [in_] + col, [out], cy(out, in_))

    def scal(out, in_, a, b, o0, o1=None):
        reads, more = [in_] + ([a] if isinstance(a, tuple) else []), ([] if o1 is None else [o1])
        add("v", lambda g, T: g.vector.tensor_scalar(ap(T, out), ap(T, in_), ap(T, a) if isinstance(a, tuple) else a, b, o0, *more), reads, [out],
            cy(out, in_, half(out, in_)))

    def both(out, x, y, op, k=2.0):
        add("v", lambda g, T: g.vector.tensor_tensor(ap(T, out), ap(T, x), ap(T, y), op), [x, y], [out], cy(out, x, k))

    def scan(out, x, y, o0, o1):
        add("v", lambda g, T: g.vector.tensor_tensor_scan(ap(T, out), ap(T, x), ap(T, y), 0.0, o0, o1), [x, y], [out], cy(out, y, half(out, y)))

    def sign(out, in_, bias=None, acc=None):
        add("a", lambda g, T: g.scalar.activation(ap(T, out), ap(T, in_), ACT.Sign, bias=ap(T, bias) if bias else 0.0, scale=-1.0,
                                                  accum_out=ap(T, acc) if acc else None), [in_] + [bias] * bool(bias), [out] + [acc] * bool(acc),
            cy(out, in_) + 0.02 * bool(acc))

    def mm(*terms, cut=(), onto=False, last=True):
        name = now[1]
        for lo, hi in zip((0,) + cut, cut + (len(terms),)):
            def fn(g, T, lo=lo, hi=hi):
                for i in range(lo, hi):
                    r = g.tensor.matmul(*[ap(T, z) for z in terms[i]], i == 0 and not onto, last and i == len(terms) - 1)
                return r
            cost = sum(C["mm"] + max(64, width(t[2])) * C["pe"] * (1 if narrow(t[2]) else 4) for t in terms[lo:hi])
            step(name, "." + str(lo) if cut else "")
            add("p", fn, [r for t in terms[lo:hi] for r in t[1:]], [terms[0][0]], cost)
        step(name)

    def plus(o, i):
        return (o, R("KR", 128 * i, 128 * i + 128, 1, 64, 65), R("E", 0, width(o), 1, 64, 65))

    def pick(r, pat, op, x, base, cm):
        add("g", lambda g, T: g.affine_select(ap(T, r), ap(T, r), pat, op, x, base, cm), [r], [r], 0.17 + 2 * C["cyc"] * width(r))

    def iota(r, pat, base, cm):
        add("g", lambda g, T: g.iota(ap(T, r), pat, base, cm, allow_small_or_imprecise_dtypes=True), [], [r], 0.13 + 2 * C["cyc"] * width(r))

    load("s", R("fr_s", 0, 16), "fr", 0, 16, 8192)
    for b in range(2):
        load("a", R("up_s", b * S, b * S + B), "up", b * B, b * B + B, 512 * B)
    for lo, hi in ((0, V // 4), (V // 4, V)):
        load("s", R("w0", lo, hi), "rec", lo, hi, 256 * (hi - lo))
    for b in range(2, F):
        load("s", R("up_s", b * S, b * S + B), "up", b * B, b * B + B, 512 * B)
    for b0, b1 in [u[:2] for u in UNITS if F <= u[0] < NO]:
        load("s", R("up_s", M0 + b0 * B, M0 + b1 * B), "up", b0 * B, b1 * B, 512 * B * (b1 - b0))
    for d in range(D):
        load("s", R("up_s", GH + d * S, GH + d * S + B), "up", V + d * B, V + d * B + B, 512 * B)

    whole = lambda n: R(n, 0, SCRATCH[n][1][1])
    nx = 128 * len(UNITS)
    for n, x in (("ID", 1.0), ("AP", 1.0), ("E", 1.0), ("WS", 0.0), ("WM", 0.0), ("EG", 1.0)):
        fill(whole(n), x)
    iota(R("kI", 0, 1), [[0, 1]], 0, 1)
    pick(whole("ID"), [[-1, 128]], OP.is_equal, 0.0, 0, 1)
    iota(R("TB", 0, F), [[S, F]], 0, 0)
    iota(R("TB", F, NO), [[B, NO - F]], F * B, 0)
    iota(R("TB", NO, NO + F), [[B, F]], 0, 0)
    iota(whole("dm"), [[16, 16]], V, 1)
    pick(whole("AP"), [[-16, 8], [0, 16]], OP.is_ge, 0.0, 0, 1)
    pick(whole("AP"), [[16, 8], [0, 16]], OP.is_ge, 0.0, 15, -1)
    pick(R("E", 0, 1024, 1, 0, 64), [[1, 64], [0, 16]], OP.is_equal, 0.0, 0, -1)
    fill(R("XT", 0, nx, 1, 64, 96), -0.25)
    fill(R("XT", 0, nx, 1, 0, 64), 0.0)
    scal(R("kI", 1, 2), R("kI", 0, 1), 15, None, OP.bitwise_and)
    fill(R("XT", 15, nx, 16, 64, 96), 1.0)
    fill(R("w0", V, W0), 0.0)
    copy("v", R("kc", 0, 1), R("kI", 1, 2))
    scal(R("kc", 1, 2), R("kI", 1, 2), 0.5, None, OP.add)
    scal(R("kc", 2, 3), R("kI", 1, 2), 15.0, None, OP.is_equal)
    for at in [b * S + B for b in range(F)]:
        copy("v", R("up_s", at, at + 16), whole("dm"))
    for i, (note, mark) in enumerate(((0.5, 0.0), (-0.5, 0.0), (-128.0, -2304.0), (256.0, 384.0), (0.0, -1.0))):
        scal(R("kc", 3 + i, 4 + i), R("kc", 2, 3), mark - note, note, OP.mult, OP.add)
    for i, x in enumerate(ROWS):
        fill(R("KR", 128 * i, 128 * i + 128), x)
    copy("a", whole("IF"), whole("ID"))
    copy("a", R("WM", 15, 128, 16), R("ID", 15, 128, 16))
    copy("a", R("WS", 15, 128, 16), R("AP", 15, 128, 16))
    copy("a", whole("LP"), whole("AP"))
    for out, in_, by in (("HI", "ID", 3), ("NI", "ID", 4), ("HF", "ID", 3), ("W1", "WS", 5), ("W2", "WS", 6), ("BP", "AP", 2), ("BN", "AP", 7),
                         ("I16", "ID", 16.0), ("AN", "AP", -1.0)):
        times(whole(out), whole(in_), by)
    for i, (r, x) in enumerate(((whole("MK"), 1.0), (whole("ON"), 1.0), (whole("rk"), 0.0), (R("w1", V, W0), 0.0), (R("ST", 0, B), 0.0),
                                (R("ST", B, S), 1.0), (R("MK", 0, B, BL), 0.0))):
        step("spare", i)
        fill(r, x)
    step("others")
    for at in [M0 + V] + [GH + d * S + B for d in range(D)]:
        copy("g", R("up_s", at, at + 16), whole("dm"))
    step("ghostE")
    pick(R("EG", 0, 768, 1, 0, 64), [[PW, D], [1, 16], [0, 16]], OP.is_equal, 0.0, 0, -1)
    step("later")
    pick(whole("LP"), [[-1, 128]], OP.is_gt, 0.0, 0, 1)
    iota(whole("CB"), [[BL, NO], [0, BL]], 0, 0)
    iota(whole("KC"), [[0, NO], [1, 16]], 0, 0)
    iota(whole("TJ"), [[-B, NO]], V - B, 0)
    step("latest")
    times(whole("LN"), whole("LP"), -1.0)
    step("jump")
    scal(whole("J"), whole("TJ"), R("kc", 0, 1), None, OP.add)
    for j in range(4):
        step("fill", j)
        copy(FILL[j], R("w1", j * V // 4, (j + 1) * V // 4), R("w0", j * V // 4, (j + 1) * V // 4))

    def marks(w, gi=1):
        b0, b1, t = F, NO, "p2"
        o = R(t, 0, BL * (b1 - b0))
        step("marks", gi)
        mm(*[(o, R("WM", 15 - j, 143 - j), R("w%d" % (w % 2), b0 * B + j, b1 * B, 16)) for j in range(16)], cut=(4, 8, 12))
        step("keep", gi)
        copy(KEEP, R("m%d" % (w % 2), b0 * BL, b1 * BL), o)

    def before(w, b):
        t, at = FRESH[b]
        step("stale", b)
        mm((R(t, at, at + S), R("E", 0, 128, 1, 64, 65), R("ST", 0, S, 1, 64, 65)),
           (R(t, at, at + B), whole("BN"), R("w%d" % ((w + 1) % 2), b * B, b * B + B)), last=False)

    def first(w, b):
        t, at = FRESH[b]
        step("fresh", b)
        mm((R(t, at, at + B), whole("BP"), R("w%d" % (w % 2), b * B, b * B + B)), onto=True)
        step("scan", b)
        scan(R("r1", b * S, b * S + S), whole("ON"), R(t, at, at + S), OP.mult, OP.add)
        step("tally", b)
        sign(R("junk", b * S, b * S + S), R("r1", b * S, b * S + S), R("kc", 1, 2), R("sums", b, b + 1))
        step("lu", b)
        scal(R("lu", b, b + 1), R("sums", b, b + 1), 0.5, float(S // 2 + S * b), OP.mult, OP.add)
        step("lx", b)
        scal(R("lx", b, b + 1), R("sums", b, b + 1), 0.5, float(S // 2 + B * b), OP.mult, OP.add)

    def frontier(w, gi=1):
        b0, b1, t, t2, at = F, NO, "p2", "p2", 512
        lo, hi, n = b0 * BL, b1 * BL, BL * (b1 - b0)
        new, was = R("m%d" % (w % 2), lo, hi), R("m%d" % ((w - 1) % 2), lo, hi)
        tot, rest = R(t2, at, at + n), R(t2, at + 256, at + 256 + n)
        step("runs", gi)
        mm((tot, whole("AN"), was), (tot, whole("AP"), new))
        mm((rest, whole("LP"), was), (rest, whole("LN"), new))
        step("cum", gi)
        scan(R("cum", lo, hi), R("MK", lo, hi), tot, OP.mult, OP.add)
        step("le", gi)
        scal(R("le", lo, hi), R("cum", lo, hi), R("kc", 0, 1), None, OP.is_le)
        step("rank", gi)
        both(R("rk", lo, hi), rest, R("cum", lo, hi), OP.add, 1.0)
        step("run", gi)
        scan(R("hi", lo, hi), R("CB", lo, hi), R("le", lo, hi), OP.max, OP.add)
        run = R("hi", lo + BL - 2, hi, BL)
        step("runlist", gi)
        copy("v", R("i16", b0, b1), run)
        step("empty", gi)
        both(R("ej", b0, b1), R("le", lo + BL - 1, hi, BL), R("J", b0, b1), OP.mult)
        step("within", gi)
        both(R("c2", b0 * 16, b1 * 16), ("at", R("rk", 0, hi), R("i16", b0, b1)), R("KC", b0 * 16, b1 * 16), OP.is_le)
        o = R(t, 0, b1 - b0)
        step("place", gi)
        mm(*([(o, whole("I16"), run), (o, whole("IF"), R("ej", b0, b1))]
             + [(o, R("WS", 15 - k, 143 - k), R("c2", b0 * 16 + k, b1 * 16, 16)) for k in range(16)]), cut=(2,))
        return o

    def wave(w):
        was, new, snd, rcv = "w%d" % (w % 2), "w%d" % ((w + 1) % 2), "snd%d" % w, "rcv%d" % w
        src = R(was, 0, W0)
        now[0] = w

        def parents(lo, hi, win):
            q = R("q16", lo * 16, hi * 16)
            step("q", lo)
            copy("v", q, ("at", win, R("lu", lo, hi)))
            step("qf", lo)
            copy(QF, R("qf", lo * 16, hi * 16), q)

        def unit(k):
            b0, b1, qs, pd, ps = UNITS[k]
            lo, hi, n = b0 * 256, b1 * 256, 16 * (b1 - b0)
            l16, h16, m = b0 * 16, b1 * 16, hi - lo
            rows, notes, by = (n, R("x", l16, h16), "HI") if b0 < NO else ((b1 - b0) * PW, R(rcv, (b0 - NO) * PW, (b1 - NO) * PW), "HF")
            step("turn", b0)
            mm((R("px", 0, 128, 1, 0, rows), notes, whole(by)))
            step("xt", b0)
            copy(XQ[2 * k + 1], R("XT", k * 128, k * 128 + 128, 1, 0, rows), R("px", 0, 128, 1, 0, rows))
            od = R("old", lo, hi)
            step("old", b0)
            copy(qs[0], od, ("at", src, R("q16", l16, h16)))

            def spread(t, at, by, rounds):
                for a in range(0, m, 512):
                    z = min(a + 512, m)
                    o = R(t, at + a, at + z)
                    mm(*([(o, R("XT", k * 128, k * 128 + 128, 1, 0, 65), R("EG" if b0 >= NO else "E", a, z, 1, 0, 65)),
                          (o, whole(by), R("old", lo + a, lo + z))] + [plus(o, 0)] * rounds))
                return R(t, at, at + m)
            if qs[1] == "a":
                step("diff", b0)
                s = spread(*pd, "NI", False)
                step("cmp", b0)
                sign(R("cb", lo, hi), s)
            step("sum", b0)
            s = spread(*ps, "HI", qs[2] == "a")
            if qs[1] == "v":
                for a in range(0, m, CUT):
                    step("cmp", b0 + a // 256)
                    z = min(a + CUT, m)
                    both(R("cb", lo + a, lo + z), R("old", lo + a, lo + z), R(s[0], s[1] + a, s[1] + z), OP.is_le, 1.0)
            step("val", b0)
            if qs[2] == "a":
                copy("a", R("val", lo, hi), s, -BIG)
            else:
                for a in range(0, m, CUT):
                    step("val", b0 + a // 256)
                    z = min(a + CUT, m)
                    scal(R("val", lo + a, lo + z), R(s[0], s[1] + a, s[1] + z), BIG, BIG, OP.add, OP.subtract)
            o = R("pc", 0, n)
            step("count", b0)
            mm(*([(o, R("W1" if qs[1] == "a" else "W2", 15 - i, 143 - i), R("cb", lo + i, hi, 16)) for i in range(16)]
                 + [plus(o, 1), plus(o, 2), (o, whole("IF"), R("qf", l16, h16))]))
            step("aim", b0)
            copy("v", R("o16", l16, h16), o)
            for b in range(b0, b1):
                step("put", b)
                copy("v", ("at", whole(new), R("o16", b * 16, b * 16 + 16)), R("val", b * 256, b * 256 + 256))

        if w == 0:
            step("place", 0)
            both(R("tu", 0, NO), whole("fr_s"), R("TB", 0, NO), OP.add)
            both(R("tu", NO, NO + F), R("fr_s", 0, F), R("TB", NO, NO + F), OP.add)
            step("list", 0)
            copy("v", R("lu", 0, NO), R("tu", 0, NO))
            copy("v", R("lx", 0, F), R("tu", NO, NO + F))
        else:
            for b in range(F):
                before(w, b)
            for j, (lo, hi, q) in enumerate(COPY):
                step("copy", j)
                copy(q, R(new, lo, hi), R(was, lo, hi))
            for b in range(F):
                first(w, b)
        early = [k for k, u in enumerate(UNITS) if u[0] < F]
        for k in early:
            b0, b1 = UNITS[k][:2]
            parents(b0, b1, R("up_s", 0, b1 * S))
            step("x", b0)
            copy(XQ[2 * k], R("x", b0 * 16, b1 * 16), ("at", R(was, 0, b1 * B + 16 * (w > 0)), R("lx", b0, b1)))
        step("tell")
        copy(TELL[0], R(snd, 16, D * PW, PW), R("lu", 0, D))
        step("send")
        for d in range(D):
            copy("g", R(snd, d * PW, d * PW + 16), R("x", d * 16, d * 16 + 16))
        add("g", w, [whole(snd)], [whole(rcv)], C["call"], 0, C["lat"] + 4.0 * (w == 0))
        if w:
            marks(w)
            node = frontier(w)
        for k in early:
            unit(k)
        if w:
            step("list", 1)
            copy("v", R("lu", F, NO), node)
        for b0, b1 in [(F, NO)] if w else [u[:2] for u in UNITS if F <= u[0] < NO]:
            parents(b0, b1, R("up_s", M0, GH if w else M0 + b1 * B))
        step("x", F)
        copy(XQ[2 * len(early)], R("x", F * 16, NO * 16), ("at", src, R("lu", F, NO)))
        for k in [k for k, u in enumerate(UNITS) if F <= u[0] < NO]:
            unit(k)
        step("heard")
        copy(TELL[1], R("lu", NO, NB), R(rcv, 16, D * PW, PW))
        parents(NO, NB, R("up_s", GH, UP))
        for k in [k for k, u in enumerate(UNITS) if NO <= u[0]]:
            unit(k)
        if w == 0:
            marks(0)

    for w in range(WAVES):
        wave(w)
    now[0] = WAVES
    for j, q in enumerate("sa"):
        o = R("w%d" % (WAVES % 2), j * V // 2, (j + 1) * V // 2)
        add(q, lambda g, T, o=o, q=q: (g.sync if q == "s" else g.scalar).dma_start(T.y[:, o[1]:o[2]], ap(T, o)), [o], [], 0.06, 128 * V)
    return ops


def order(ops):
    def turn(i):
        w, name = ops[i]["at"]
        names = ORDER[min(w, 1)].split() if w < WAVES else []
        return (w, names.index(name) if name in names else -1, i)
    out, left = [], sorted(range(len(ops)), key=turn)
    done = set()
    while left:
        i = [i for i in left if done.issuperset(ops[i]["deps"])][0]
        left.remove(i)
        done.add(i)
        out.append(i)
    return out


def rank_program(g, core, T, topo):
    rank = T.rank_of(core)
    if rank is None:
        return
    ops = plan()
    seq = order(ops)
    queue = {"v": g.vector, "a": g.scalar, "p": g.tensor, "g": g, "s": g.sync}
    watched, last = [False] * len(ops), {}
    for o in ops:
        for j, must in o["deps"].items():
            watched[j] = watched[j] or must
    for i in seq:
        last[ops[i]["q"]] = i
    dsts, eng, used = [T.cores[(rank + d) % N] for d in range(1, D + 1)], {}, []
    for z in sorted(dsts, key=lambda z: len(topo.engines(core, z))):
        eng[z] = [e for e in topo.engines(core, z) if e not in used][:4]
        used = used + eng[z]
    tok, total, waited, seen, nd = {}, {}, {}, {}, 0
    for i in seq:
        o, req = ops[i], {}
        q = o["q"]
        for j, must in o["deps"].items():
            if must:
                s, v = tok[j]
                req[s] = max(req.get(s, 0), v)
        for s in sorted(req):
            if seen.get((q, s), 0) < req[s]:
                queue[q].wait_ge(T.sem[s], req[s])
                seen[(q, s)] = req[s]
                waited[s] = max(waited.get(s, 0), req[s])
        if isinstance(o["fn"], int):
            w, tr = o["fn"], []
            for d, z in enumerate(dsts):
                rid, pid, _ = topo.addr(z)
                src, dst = message(T, T, w, d)
                tr.append(RemoteDMATransfer(dst_ids=[DstId(rid=rid, pnc=pid)], dma_engine_mask=sum(1 << e for e in eng[z]), remote_sem=T.sem["gh%d" % w],
                                            src=src, dst=dst))
            g.remote_dma_fused(tr, local_sem=T.sem.sent)
            total["sent"] = total.get("sent", 0) + sum(len(eng[z]) for z in dsts)
            tok[i] = ("gh%d" % w, 4 * D)
            total["gh%d" % w] = 4 * D
            continue
        r = o["fn"](g, T)
        if o["dma"]:
            s, nd = "d%d" % nd, nd + 1
            r.then_inc(T.sem[s], 16)
            total[s] = 16
            tok[i] = (s, 16)
        elif watched[i] or last[q] == i:
            s = "s" + q
            total[s] = total.get(s, 0) + 1
            r.then_inc(T.sem[s], 1)
            tok[i] = (s, total[s])
    for s in total:
        if waited.get(s, 0) < total[s]:
            g.wait_ge(T.sem[s], total[s])
